import numpy as np, ml_dtypes
CORES = [8,136,40,168]
N = 4
BF = ml_dtypes.bfloat16
def gentries(a):
    return np.ascontiguousarray(a.reshape(8, 16, -1).transpose(0, 2, 1)).reshape(8, -1)
def gtable(e):
    e = np.asarray(e); return np.ascontiguousarray(e.reshape(8, -1, 16).transpose(0, 2, 1)).reshape(128, -1).astype(np.int32)
V, G, L, D, RO = 3072, 128, 512, 6, 3
S = (N - 1) * G; W = V + S
def weave(rng, share, ring=0.03, ends=False, most=V):
    o = rng.permutation(V); b = rng.random(V) < share; b[0] = True
    if ends: o = np.concatenate([np.array([0, V - 1]), rng.permutation(np.arange(1, V - 1))]); b[1:4] = True
    st = np.flatnonzero(b); en = np.append(st[1:], V) - 1; T = len(st); top = o[st]; last = o[en]
    par = np.empty(V, np.int64); side = np.zeros(V, np.int64); kd = np.full(V, W, np.int64)
    par[o[1:]] = o[:-1]
    w = rng.permutation(T); gp = rng.permutation(S); n = min((T + 1) // 2, int(rng.integers(S // 2, S + 1)), most)
    if ends: w = np.concatenate([np.array([0, 1]), 2 + rng.permutation(T - 2)]); gp = np.concatenate([np.array([0, S - 1]), 1 + rng.permutation(S - 2)])
    par[top[w[:n]]] = V + gp[:n]; side[top[w[:n]]] = rng.integers(0, 2, n)
    c = w[n:]; z = rng.random(len(c)) < ring
    par[top[c[z]]] = last[c[z]]
    e = c[~z]; v = rng.permutation(V)
    if ends:
        for i in range(min(4, len(e))):
            j = int(np.flatnonzero(v == top[e[i]])[0]); h = v[i]; v[i] = v[j]; v[j] = h
    v = v[:len(e)]; par[top[e]] = v; side[top[e]] = 1; kd[v] = top[e]
    return par, side, kd
def pairs(rng, share, coin, classes=False):
    h = V // 2; o = rng.permutation(V)
    if classes: o = o[np.argsort(-((o - int(rng.integers(0, 16))) % 16), kind="stable")]; o[:h] = rng.permutation(o[:h])
    a, f = o[:h], o[h:]; b = rng.random(h) < share; b[0] = True
    st = np.flatnonzero(b); en = np.append(st[1:], h) - 1; T = len(st)
    par = np.empty(V, np.int64); side = np.zeros(V, np.int64); kd = np.full(V, W, np.int64)
    par[a[1:]] = a[:-1]; par[f] = a
    mid = np.ones(h, bool); mid[en] = False; j = np.flatnonzero(mid); c = rng.random(len(j)) < coin
    side[f[j]] = np.where(c, 0, 1); side[a[j + 1]] = np.where(c, 1, 0); kd[a[j]] = np.where(c, a[j + 1], f[j])
    w = rng.permutation(T); n = min((T + 1) // 2, int(rng.integers(S // 2, S + 1))); top = a[st]
    side[top] = 1; par[top[w[:n]]] = V + rng.permutation(S)[:n]; side[top[w[:n]]] = rng.integers(0, 2, n)
    e = a[en][rng.permutation(T)[:T - n]]; par[top[w[n:]]] = e; kd[e] = top[w[n:]]
    return par, side, kd, a, f
def comb(rng, T):
    R = 8; m = min(D, 5); n = T - R; q = V - R * m; big = min(n, (q - 2 * n) // (D - 2)); rest = q - 2 * n - big * (D - 2)
    ln = np.full(n, 2, np.int64); ln[:big] = D
    if big < n: ln[big] += rest; rest = 0
    ln = np.concatenate([np.full(R, m, np.int64), rng.permutation(ln), np.ones(rest, np.int64)])
    o = rng.permutation(V); en = np.add.accumulate(ln) - 1; top = o[en - ln + 1]; last = o[en]
    par = np.empty(V, np.int64); side = np.zeros(V, np.int64); kd = np.full(V, W, np.int64)
    par[o[1:]] = o[:-1]
    free = np.ones(V, bool); free[o[:R * m]] = False; free[last[:T]] = False; a = rng.permutation(np.flatnonzero(free))
    par[top[:R]] = last[:R]; side[top[:R]] = 1; kd[last[:R]] = top[:R]
    t = rng.permutation(top[R:]); w = int(rng.integers(S // 2, S + 1))
    par[t[:w]] = V + rng.permutation(S)[:w]; side[t[:w]] = rng.integers(0, 2, w)
    e = t[w:]; v = a[:len(e)]; par[e] = v; side[e] = 1; kd[v] = e
    off = np.zeros(V, np.int64); off[last[:T]] = 4
    for k in range(1, m): off[o[en[:R] - k]] = max(0, 4 - (m - k))
    sg = np.empty((16, V), np.int64); sg[:, o] = np.repeat(2 * rng.integers(0, 2, (16, len(ln))) - 1, ln, axis=1)
    return par, side, kd, a, np.where(free[None, :], rng.integers(0, 2, (16, V)), sg * off[None, :])
def knit(z):
    return [np.stack([np.stack([z[q][g][i] for g in range(8)]) for q in range(N)]) for i in range(3)]
def shown(rng):
    return np.ascontiguousarray(np.argsort(rng.random((N, 8, V)), axis=-1)[..., :S]).reshape(N, 8, N - 1, G)
def seen(x, sl):
    z = []
    for r in range(N):
        w = [x[r]]
        for d in range(1, N):
            q = (r - d) % N; w.append(np.take_along_axis(x[q], sl[q][:, d - 1][:, None, :], 2))
        z.append(np.concatenate(w, axis=2))
    return np.stack(z)
def gaps(full, par):
    return np.add.reduce(np.abs(full[..., :V] - np.take_along_axis(full, par[:, :, None, :], 3)), axis=2)
def level(v, share):
    s = np.sort(v, axis=-1); n = v.shape[-1]; i = np.clip(((1 - share) * n).astype(np.int64), 0, n - 1)
    return np.take_along_axis(s, i[..., None], 2)[..., 0]
def numbers16(rng):
    u = rng.random((N, 8, 16, V)) ** np.exp2(rng.integers(-1, 2, (N, 8, 1, V)))
    return np.minimum(np.floor(16 * u), 15).astype(np.int64)
def pack(x, par, side, kd, sl, th, A):
    return {"x": np.ascontiguousarray(x.reshape(N, 128, V)).astype(np.float32).astype(BF), "hang": np.stack([gtable(a) for a in 2 * par + side]), "kid": np.stack([gtable(a) for a in kd]),
            "shw": np.stack([gtable(a.reshape(8, -1)) for a in sl]), "bar": np.repeat(np.stack([th, A], axis=-1), 16, axis=1).astype(np.int32)}
def setup_inputs(rng):
    sh = rng.choice(np.array([0.15, 0.25, 0.4]), (N, 8))
    par, side, kd = knit([[weave(rng, sh[q, g]) for g in range(8)] for q in range(N)]); sl = shown(rng); x = numbers16(rng)
    th = level(gaps(seen(x, sl), par), rng.choice(np.array([0.1, 0.2, 0.35, 0.6]), (N, 8)))
    A = level(np.add.reduce(x, axis=2), rng.choice(np.array([0.02, 0.08, 0.2]), (N, 8)))
    return pack(x, par, side, kd, sl, th, A)
def setup_inputs_room(rng):
    h = V // 2; b = rng.integers(4, 12, (8, 16, 1)); th = rng.integers(8, 41, (N, 8))
    A = np.add.reduce(b[:, :, 0], axis=1)[None, :] + rng.choice(np.array([0, 1, 1, 16]), (N, 8))
    x = np.empty((N, 8, 16, V), np.int64); sl = np.empty((N, 8, N - 1, G), np.int64); z = []
    for q in range(N):
        z.append([])
        for g in range(8):
            k = pairs(rng, 0.3, 0.5, g > 5); z[q].append(k); a, f = k[3], k[4]
            sl[q, g] = rng.permutation(a)[:S].reshape(N - 1, G)
            n = int(rng.choice(np.array([0, 1, L - 1, L, L + 1, h])))
            if q < 2: n = (L, L + 1, h, L - 1, 1, 0, L, L + 1)[(g + q) % 8]
            t0 = int(th[q, g]); coin = rng.random(h) < 0.5; hit = (np.arange(h) if g > 5 else rng.permutation(h)) < n
            t = np.where(hit, np.where(coin, t0, rng.integers(t0, 64, h)), np.where(coin, t0 - 1, rng.integers(0, t0, h)))
            size = (t[None, :] + (np.arange(16)[:, None] + rng.integers(0, 16, h)[None, :]) % 16) // 16
            v = np.repeat(b[g], V, axis=1); v[:, f] = b[g] + size * (2 * rng.integers(0, 2, (16, h)) - 1); x[q, g] = v
    par, side, kd = knit(z)
    return pack(x, par, side, kd, sl, th, A)
def setup_inputs_deep(rng):
    few = min(L, -(-V // D)); z = []
    for q in range(N): z.append([weave(rng, 0.04, 0.3) if g % 4 == 0 else pairs(rng, 0.02, 0.0) if g % 4 == 1 else comb(rng, L if g % 4 == 2 else few) for g in range(8)])
    par, side, kd = knit(z); sl = shown(rng); x = numbers16(rng); b = rng.integers(4, 12, (8, 16, 1))
    for q in range(N):
        for g in (2, 3, 6, 7):
            x[q, g] = b[g] + z[q][g][4]; sl[q, g] = rng.permutation(z[q][g][3])[:S].reshape(N - 1, G)
    th = level(gaps(seen(x, sl), par), rng.choice(np.array([0.03, 0.06, 0.1]), (N, 8)))
    th[:, np.array([2, 3, 6, 7])] = rng.integers(17, 49, (N, 4))
    return pack(x, par, side, kd, sl, th, np.full((N, 8), 255))
def setup_inputs_ends(rng):
    par, side, kd = knit([[weave(rng, 0.3, 0.2, True) for g in range(8)] for q in range(N)]); sl = np.empty((N, 8, N - 1, G), np.int64)
    for q in range(N):
        for g in range(8): sl[q, g] = np.concatenate([np.array([0]), rng.permutation(np.arange(1, V - 1))[:S - 2], np.array([V - 1])]).reshape(N - 1, G)
    x = np.repeat(15 * rng.integers(0, 2, (N, 8, 1, V)), 16, axis=2)
    odd = (rng.random((N, 8, 1, V)) < 0.3) & (np.arange(16)[:, None] == rng.integers(0, 16, (N, 8, 1, V)))
    x = np.where(odd, np.abs(x - 1), x)
    th = rng.choice(np.array([0, 1, 239, 240, 241]), (N, 8)); A = rng.choice(np.array([0, 1, 239, 240, 241, 255]), (N, 8))
    th[0] = np.array([0, 1, 239, 240, 240, 0, 239, 1]); A[0] = np.array([241, 240, 239, 241, 0, 1, 241, 240])
    return pack(x, par, side, kd, sl, th, A)
def setup_inputs_afar(rng):
    sh = rng.choice(np.array([0.2, 0.3, 0.4]), (N, 8))
    par, side, kd = knit([[weave(rng, sh[q, g]) for g in range(8)] for q in range(N)]); sl = shown(rng)
    for q in range(N):
        sl[q, 1] = ((V // 16) * int(rng.integers(0, 9)) + rng.permutation(S)).reshape(N - 1, G)
        v = np.argsort((np.arange(V) - int(rng.integers(0, 16))) % 16, kind="stable")[:S]; sl[q, 4] = rng.permutation(v).reshape(N - 1, G)
    b = np.empty((N, 8, 16, 1), np.int64)
    for g in range(8):
        o = rng.permutation(16)
        for q in range(N): b[q, g, :, 0] = [13 if bin(int(i) & (q + 1)).count("1") % 2 else 2 for i in o]
    x = b + rng.integers(0, 2, (N, 8, 16, V))
    th = rng.choice(np.array([17, 40, 80, 90]), (N, 8)); th[rng.integers(0, N, 8), np.arange(8)] = rng.integers(242, 256, 8)
    return pack(x, par, side, kd, sl, th, rng.choice(np.array([128, 255, 255]), (N, 8)))
def setup_inputs_spread(rng):
    sh = 0.02 + 0.6 * rng.random((N, 8)); full = np.arange(8) % 3 == 2
    par, side, kd = knit([[weave(rng, 0.9, 0.0, False, 16) if full[g] else weave(rng, sh[q, g], 0.1) for g in range(8)] for q in range(N)]); sl = shown(rng)
    x = np.minimum(np.floor(np.exp2(4 * rng.random((N, 8, 1, V))) * (0.05 + rng.random((N, 8, 16, V)))), 15).astype(np.int64)
    th = level(gaps(seen(x, sl), par), np.where(full, 0.15, np.exp2(-6 * rng.random((N, 8)))))
    A = np.where((rng.random((N, 8)) < 0.7) | full, level(np.add.reduce(x, axis=2), np.where(full, 0.03, np.exp2(-6 * rng.random((N, 8))))), rng.integers(0, 256, (N, 8)))
    return pack(x, par, side, kd, sl, th, A)
def check_inputs(d):
    bad = []; x = np.asarray(d["x"]).astype(np.float32)
    if not np.all((x >= 0) & (x <= 15) & (x == np.floor(x))): bad.append("range of x")
    for k, lo, hi in (("hang", 0, 2 * W - 1), ("kid", 0, W), ("shw", 0, V - 1), ("bar", 0, 255)):
        if np.min(d[k]) < lo or np.max(d[k]) > hi: bad.append("range of " + k)
    b = np.asarray(d["bar"]).reshape(N, 8, 16, 2)
    if np.any(b != b[:, :, :1]): bad.append("bar not alike on a group's rows")
    if bad: return bad
    for r in range(N):
        hs, ks, ss = (gentries(np.asarray(d[k][r])).astype(np.int64) for k in ("hang", "kid", "shw"))
        for g in range(8):
            h = hs[g]; p = h >> 1; own = p < V
            if len(np.unique(h[own])) < np.count_nonzero(own): bad.append("two stitches on one side of a parent")
            if len(np.unique(p[~own])) < np.count_nonzero(~own): bad.append("two stitches under one ghost")
            m = np.flatnonzero(own & (h % 2 == 1)); want = np.full(V, W, np.int64); want[p[m]] = m
            if np.any(ks[g] != want): bad.append("kid against hang")
            if len(np.unique(ss[g])) < S: bad.append("a stitch shown twice")
    return sorted(set(bad))
def reference(x, hang, kid, shw, bar):
    now = x.astype(np.float32).astype(np.int64).reshape(N, 8, 16, V)
    h = np.stack([gentries(a) for a in hang]).astype(np.int64); par = h >> 1; side = h & 1
    kd = np.stack([gentries(a) for a in kid]).astype(np.int64); sl = np.stack([gentries(a) for a in shw]).astype(np.int64).reshape(N, 8, N - 1, G)
    th = bar[:, ::16, 0].astype(np.int64); A = bar[:, ::16, 1].astype(np.int64)
    flag = np.zeros((N, 8, V), bool)
    for rnd in range(RO):
        full = seen(now, sl)
        cand = (gaps(full, par) >= th[:, :, None]) | flag
        drop = cand & (np.add.accumulate(cand.astype(np.int64), axis=2) <= L)
        stop = np.ones((N, 8, W), bool); stop[..., :V] = drop | (np.add.reduce(now, axis=2) >= A[:, :, None])
        slot = np.zeros((N, 8, W), bool); now = now.copy(); par2 = par.copy(); side2 = side.copy(); kd2 = kd.copy()
        for r in range(N):
            for g in range(8):
                p, s, c1, st, f = par[r, g], side[r, g], kd[r, g], stop[r, g], full[r, g]
                p2, s2, c2, new = par2[r, g], side2[r, g], kd2[r, g], now[r, g]
                d = [np.flatnonzero(drop[r, g])]; live = [np.ones(len(d[0]), bool)]
                top = np.full(len(d[0]), W, np.int64)
                for k in range(D):
                    i = np.flatnonzero(live[k]); v = d[k][i]; u = p[v]
                    nxt = d[k].copy(); nxt[i] = u; go = np.zeros(len(nxt), bool); go[i] = (s[v] == 0) & ~st[u]
                    top[i] = c1[v]; d.append(nxt); live.append(go)
                anchor = d[D]; slot[r, g][anchor[anchor >= V]] = True
                up = f[:, anchor]
                for k in range(D - 1, -1, -1):
                    up = (f[:, d[k]] + up) >> 1
                    new[:, d[k][live[k]]] = up[:, live[k]]
                for k in range(D):
                    i = np.flatnonzero(live[k]); v = d[k][i]
                    if k == 0:
                        c = top[i]; has = c < V; c2[v] = c; p2[c[has]] = v[has]; s2[c[has]] = 1
                    else:
                        w = d[k - 1][i]; c = c1[w]; has = c < V
                        c2[v] = np.where(has, w, W); p2[c[has]] = v[has]; s2[c[has]] = 0; s2[w[has]] = 1
        par, side, kd = par2, side2, kd2
        flag = np.zeros((N, 8, V), bool)
        for q in range(N):
            for e in range(1, N):
                r = (q + e) % N; z = slot[r, :, V + (e - 1) * G:V + e * G]
                for g in range(8): flag[q, g][sl[q, g, e - 1][z[g]]] = True
    return {"y": now.reshape(N, 128, V).astype(np.float32).astype(BF), "yh": (2 * par + side).astype(np.float32)}

@@ -1,0 +1,648 @@
+import numpy as np
+from concourse.bass import DstId, RemoteDMATransfer
+from concourse.mybir import AluOpType, ActivationFunctionType
+
+V, W, NC, SG, RO = 3072, 3456, 192, 224, 3
+XWID = W + 3584
+TW = 16 * SG
+U0 = 8
+UW = 4 * TW
+BIG = 32768.0
+MAGIC = 12582912.0
+MAGIC1K = MAGIC * 1024.0
+CYC, PEC, GATH, SCAT, WAKE = 1.04e-3, 0.6e-3, 1.56, 3.8, 0.06
+MODELS = (((0.7, 0.45, 0.75, 1.0), 0.88), ((1.0, 1.0, 1.0, 1.0), 1.0), ((1.3, 1.55, 1.6, 1.0), 1.25))
+TRIES = 2500
+PLAN = {}
+
+F, B, I, U, H = "float32", "bfloat16", "int32", "uint16", "float16"
+
+
+def _s(n, d):
+    return ("sbuf", [128, n], d)
+
+
+SCRATCH = {
+    "xw0": _s(XWID, B), "xw1": _s(XWID, B), "at": _s(TW, B), "ut": _s(U0 + UW + 512, F), "htb": _s(6144, B),
+    "xa": _s(2048, B), "ee": _s(3584, B), "uh": _s(3584, H), "half": _s(3584, B), "ft": _s(TW, F),
+    "wrp": _s(4 * SG, F), "wrd": _s(4 * SG, F), "zero": _s(4 * SG, F),
+    "g0": _s(512, B), "g1": _s(512, B), "zz": _s(3328, F), "jc": _s(512, F), "neg": _s(512, B),
+    "hh": _s(512, B), "mt": _s(512, B), "one": _s(512, F),
+    "sh0": _s(384, B), "sh1": _s(384, B), "sh2": _s(384, B), "fw": _s(1792, F),
+    "fl0": _s(384, F), "fl1": _s(384, F), "flw": _s(SG, F), "h0": _s(SG, F),
+    "hi": _s(NC, I), "ki": _s(NC, I), "si": _s(24, I), "s2": _s(48, I), "s3": _s(24, F), "bi": _s(8, I), "bf": _s(8, F),
+    "shn": _s(24, U), "shs": _s(24, U), "pn": _s(NC, U), "hl": _s(NC, U), "xl": _s(NC, U), "tl": _s(12, U),
+    "ci": _s(3 * SG, I), "ats": _s(2 * SG, B), "fls": _s(SG, B), "sts": _s(SG, B), "own": _s(2 * SG, B),
+    "hf": _s(NC, F), "hk": _s(NC, F), "hv": _s(NC, F), "t1": _s(NC, F), "t2": _s(NC, F), "t3": _s(NC, F),
+    "t4": _s(NC, F), "t5": _s(NC, F), "t6": _s(NC, F),
+    "hs": _s(384, F), "hsh": _s(384, B), "hsl": _s(384, B),
+    "cand": _s(NC, B), "cx": _s(200, F), "val": _s(NC, F), "kc": _s(NC, B),
+    "pi": _s(8, I), "pc": _s(32, F), "oh": _s(16, F), "ia": _s(SG, F), "ib": _s(NC, F), "ic": _s(128, F),
+    "v16": _s(SG, F), "k2": _s(NC, F), "slf": _s(NC, F), "dm": _s(NC, F), "hold": _s(NC, F),
+    "ew": _s(144, F), "wset": _s(144 * 10, B), "bo": _s(128, F), "tri": _s(128, F), "idn": _s(128, F),
+    "wblk": _s(128 * 8, B),
+    "sl": _s(192, U), "nl": _s(224, U), "al": _s(192, U), "fa": _s(32, U), "a0": _s(32, U),
+    "mm": _s(192, F), "lv": _s(224, F), "ng": _s(192, F), "nf": _s(224, F),
+    "ta": _s(192, F), "tb": _s(192, F), "tc": _s(192, F), "td": _s(32, F), "dum": _s(64, F), "duf": _s(32, F),
+}
+for _k in range(8):
+    SCRATCH["b%d" % _k] = ("psum", [128, 512], F)
+NDMA = 60
+SEMAPHORES = ["cv", "ca", "cp", "cg", "sent", "sa0", "sa1", "sa2", "fa0", "fa1"] + ["d%d" % _k for _k in range(NDMA)]
+
+
+def rank_program(g, core, T, topo):
+    rank = T.rank_of(core)
+    if rank is None:
+        return
+    N = len(T.cores)
+    A = AluOpType
+    AF = ActivationFunctionType
+    Q = {"v": g.vector, "a": g.scalar, "p": g.tensor, "g": g, "s": g.sync}
+    hist = {}
+    nodes = []
+    succ = []
+
+    def R(name, a=None, b=None, s=None, row=None, cls=None):
+        t = T[name]
+        a = 0 if a is None else a
+        b = t.shape[1] if b is None else b
+        cs = slice(a, b) if s is None else slice(a, b, s)
+        pat = t[:, cs] if row is None else t[row::16, cs]
+        n = len(range(a, b, s or 1))
+        if SCRATCH[name][0] == "psum":
+            return (pat, [(name, 0, 512, "psum")], None, n, 4, True)
+        return (pat, [(name, a, b, row if cls is None else cls)], None, n, 4 if SCRATCH[name][2] in (F, I) else 2, False)
+
+    def X(win, off):
+        return (win[0].indirect(off[0]), win[1], off[1], 16 * off[3], win[4], False)
+
+    def hbm(t):
+        return (t, [], None, 0, 0, False)
+
+    def ap(o):
+        return o[0] if isinstance(o, tuple) else o
+
+    def node(opts, outs, ins, lat=0.0, kind="c", arrive=None):
+        reads, writes = [], []
+        for o in ins:
+            if isinstance(o, tuple):
+                reads += o[1] + (o[2] or [])
+        for o in outs:
+            writes += o[1]
+            reads += o[2] or []
+        me = len(nodes)
+        qs = "".join(opts)
+        deps = set()
+        for regs, wr in ((reads, False), ([] if arrive else writes, True)):
+            for (n, a, b, cls) in regs:
+                for (a2, b2, cls2, wr2, qs2, who) in hist.get(n, []):
+                    if a2 >= b or a >= b2:
+                        continue
+                    if cls == "psum":
+                        if not (wr or wr2 or qs2 != qs or len(qs) > 1):
+                            continue
+                    elif not (wr or wr2) or (cls is not None and cls2 is not None and cls != cls2):
+                        continue
+                    deps.add(who)
+        sort = 2 if qs == "p" else 1 if outs[0][2] else 0 if ins and isinstance(ins[0], tuple) and ins[0][2] else 3
+        nodes.append({"sort": sort, "opts": opts, "lat": lat, "kind": kind, "deps": sorted(deps), "arrive": arrive})
+        for (n, a, b, cls) in writes:
+            h = [e for e in hist.get(n, []) if not (a <= e[0] and e[1] <= b and (cls is None or cls == e[2]))]
+            hist[n] = h + [(a, b, cls, True, qs, me)]
+        for (n, a, b, cls) in reads:
+            hist[n] = hist.get(n, []) + [(a, b, cls, False, qs, me)]
+
+    def vcost(out, ins, per):
+        if out[2]:
+            return 0.05 + out[3] * SCAT * CYC
+        if ins and ins[0][2]:
+            return 0.05 + out[3] * GATH * CYC
+        return max(64, out[3] * per) * CYC
+
+    def half(*o):
+        return 0.5 if all(x[4] == 2 for x in o) else 1.0
+
+    def aopt(out, in_, f, bias, scale):
+        return (vcost(out, [in_], 1.0) + 0.02, lambda: g.scalar.activation(out[0], in_[0], f, ap(bias), ap(scale)))
+
+    def cp(out, in_, either=False):
+        opts = {"v": (vcost(out, [in_], half(out, in_)), lambda: g.vector.tensor_copy(out[0], in_[0]))}
+        if either:
+            opts["a"] = aopt(out, in_, AF.Identity, 0.0, 1.0)
+        node(opts, [out], [in_])
+
+    def lin(out, in_, scale, bias):
+        node({"v": (vcost(out, [in_], half(out, in_)), lambda: g.vector.tensor_scalar(out[0], in_[0], ap(scale), ap(bias), A.mult, A.add)),
+              "a": aopt(out, in_, AF.Identity, bias, scale)}, [out], [in_, scale, bias])
+
+    def tt(out, a, b, op):
+        node({"v": (vcost(out, [a], 1.0 if a[5] or b[5] else 2.0), lambda: g.vector.tensor_tensor(out[0], a[0], b[0], op))}, [out], [a, b])
+
+    def ts(out, a, s1, op0, s2=None, op1=None):
+        c = vcost(out, [a], half(out, a))
+        if op1 is None:
+            node({"v": (c, lambda: g.vector.tensor_scalar(out[0], a[0], ap(s1), None, op0))}, [out], [a, s1])
+        else:
+            node({"v": (c, lambda: g.vector.tensor_scalar(out[0], a[0], ap(s1), ap(s2), op0, op1))}, [out], [a, s1, s2])
+
+    def scan(out, d0, d1, init, op0, op1):
+        node({"v": (vcost(out, [], half(out, d0, d1)), lambda: g.vector.tensor_tensor_scan(out[0], d0[0], d1[0], init, op0, op1))},
+             [out], [d0, d1])
+
+    def fill(out, c):
+        node({"v": (vcost(out, [], half(out)), lambda: g.vector.memset(out[0], c))}, [out], [])
+
+    def act(out, in_, func=None, bias=0.0, scale=1.0):
+        node({"a": aopt(out, in_, AF.Identity if func is None else func, bias, scale)}, [out], [in_, bias, scale])
+
+    def sput(o, z, either=False):
+        opts = {"a": (vcost(o, [z], 1.0), lambda: g.scalar.activation(o[0], z[0], AF.Silu))}
+        if either:
+            opts["v"] = (vcost(o, [z], 1.0), lambda: g.vector.tensor_copy(o[0], z[0]))
+        node(opts, [o], [z])
+
+    def iota(out, pattern, base, mult):
+        c = 0.13 + 2 * out[3] * CYC
+        if SCRATCH[out[1][0][0]][2] == I:
+            node({"g": (c, lambda: g.iota(out[0], pattern, base, mult))}, [out], [])
+        else:
+            node({"g": (c, lambda: g.iota(out[0], pattern, base, mult, allow_small_or_imprecise_dtypes=True))}, [out], [])
+
+    def gfill(name, a, b, c):
+        for lo in range(a, b, 1024):
+            hi = min(b, lo + 1024)
+            iota(R(name, lo, hi), [[0, hi - lo]], c, 0)
+
+    def mms(out, pairs, start=True, stop=True):
+        def make():
+            for n, (l, r) in enumerate(pairs):
+                ins = g.tensor.matmul(out[0], l[0], r[0], start and n == 0, stop and n == len(pairs) - 1)
+            return ins
+        node({"p": (sum(max(64, r[3]) for (l, r) in pairs) * PEC, make)}, [out], [x for pr in pairs for x in pr])
+
+    def dma(q, out, in_, lat=2.4):
+        node({q: (0.1, lambda: Q[q].dma_start(out[0], in_[0]))}, [out], [in_], lat=lat, kind="d")
+
+    def send(src, so, dst, off, sign, sem):
+        def make():
+            tr = []
+            for d in range(1, N):
+                peer = T.cores[(rank + sign * d) % N]
+                rid, pid = topo.addr(peer, core)
+                e = topo.engines(core, peer)
+                pick = ((0, 2), (4, 6), (1, 5))[d - 1]
+                tr.append(RemoteDMATransfer(dst_ids=[DstId(rid=rid, pnc=pid)], dma_engine_mask=(1 << e[pick[0]]) | (1 << e[pick[1]]),
+                                            remote_sem=T.sem[sem], src=T[src][:, so + (d - 1) * 128:so + d * 128],
+                                            dst=T[dst][:, off + (d - 1) * 128:off + d * 128]))
+            g.remote_dma_fused(tr, local_sem=T.sem.sent)
+        node({"g": (0.5, make)}, [R(dst, off, off + 384)], [R(src, so, so + 384)], lat=3.0, kind="r", arrive=sem)
+
+    def schedule(prio, lean):
+        left = [len(nd["deps"]) for nd in nodes]
+        free = {q: 0.0 for q in Q}
+        at, done, out = {}, {}, []
+        ready = [n for n in range(len(nodes)) if not left[n]]
+        for n in ready:
+            at[n] = 0.0
+        while ready:
+            best = []
+            for n in ready:
+                o = nodes[n]["opts"]
+                fin, q = min((max(at[n], free[q]) + o[q][0] + (lean[n] if q == "v" else 0.0), q) for q in o)
+                best.append((max(at[n], free[q]), -prio[n], n, q))
+            t0, _, n, q = min(best)
+            end = t0 + nodes[n]["opts"][q][0]
+            for (t1, p1, m, q1) in best:
+                if q1 == q and t1 < end and -p1 > prio[n] and end - p1 > t1 + nodes[m]["opts"][q][0] + prio[n]:
+                    t0, n = t1, m
+                    end = t0 + nodes[n]["opts"][q][0]
+            free[q] = end
+            done[n] = end + nodes[n]["lat"]
+            out.append((n, q))
+            ready.remove(n)
+            for s in succ[n]:
+                left[s] -= 1
+                if not left[s]:
+                    at[s] = max(done[d] for d in nodes[s]["deps"]) + WAKE
+                    ready.append(s)
+        return out
+
+    def replay(out, f):
+        free = {q: 0.0 for q in Q}
+        done = {}
+        for n, q in out:
+            nd = nodes[n]
+            t0 = max([free[q]] + [done[d] + WAKE for d in nd["deps"]])
+            free[q] = t0 + nd["opts"][q][0] * f[nd["sort"]]
+            done[n] = free[q] + nd["lat"]
+        return max(done.values())
+
+    def plan():
+        base = [0.0] * len(nodes)
+        for n in range(len(nodes) - 1, -1, -1):
+            base[n] = min(c for c, _ in nodes[n]["opts"].values()) + nodes[n]["lat"] + max([base[s] + WAKE for s in succ[n]] + [0.0])
+        rng = np.random.RandomState(7)
+        shift, lean = np.zeros(len(nodes)), np.full(len(nodes), 0.8)
+        best = None
+        for it in range(TRIES):
+            s2, l2 = shift.copy(), lean.copy()
+            if it:
+                pick = rng.rand(len(nodes)) < 0.015
+                s2[pick] += rng.randn(int(pick.sum())) * 1.5
+                pick = rng.rand(len(nodes)) < 0.03
+                l2[pick] = rng.randn(int(pick.sum())) * 1.5
+            out = schedule([float(b + s) for b, s in zip(base, s2)], [float(x) for x in l2])
+            score = sum(replay(out, f) / w for f, w in MODELS)
+            if best is None or score <= best[0]:
+                best, shift, lean = (score, out), s2, l2
+        return best[1]
+
+    def emit():
+        for n, nd in enumerate(nodes):
+            succ.append([])
+            for d in nd["deps"]:
+                succ[d].append(n)
+        if "order" not in PLAN:
+            PLAN["order"] = plan()
+        where, mark, final = {}, {}, {}
+        cnt = {q: 0 for q in Q}
+        seen = {q: {} for q in Q}
+        ndma = nsent = 0
+        for n, q in PLAN["order"]:
+            nd = nodes[n]
+            need = {}
+            for d in nd["deps"]:
+                if not (q == "p" and where[d] == "p"):
+                    need[mark[d][0]] = max(need.get(mark[d][0], 0), mark[d][1])
+            for sem in need:
+                if seen[q].get(sem, 0) < need[sem]:
+                    Q[q].wait_ge(T.sem[sem], need[sem])
+                    seen[q][sem] = need[sem]
+            ins = nd["opts"][q][1]()
+            if nd["kind"] == "c":
+                cnt[q] += 1
+                mark[n] = ("c" + q, cnt[q])
+                ins.then_inc(T.sem["c" + q], 1)
+            elif nd["kind"] == "d":
+                mark[n] = ("d%d" % ndma, 16)
+                ins.then_inc(T.sem["d%d" % ndma], 16)
+                ndma += 1
+            else:
+                mark[n] = (nd["arrive"], 2 * (N - 1))
+                nsent += 2 * (N - 1)
+                final["sent"] = nsent
+            final[mark[n][0]] = mark[n][1]
+            where[n] = q
+        for sem in final:
+            g.wait_ge(T.sem[sem], final[sem])
+
+    def ws(n, i):
+        return R("wset", 144 * n + 15 - i, 144 * n + 143 - i)
+
+    def wb(n):
+        return R("wblk", 128 * n, 128 * n + 128)
+
+    def wrap(n, name, a, b):
+        return [(ws(n, i), R(name, a + i, b, 16)) for i in range(16)]
+
+    SUM, SIG, NAT, FL, FL0, NP, CH, CM, ZH, ZM = range(10)
+    IDN, NID, TRV, TRU, ONE, NON, KV, KW = range(8)
+    xw = ["xw0", "xw1"]
+    col = lambda k: R("pc", k, k + 1)
+    oh = lambda k: R("oh", k, k + 1)
+    urow = lambda k: R("ut", U0, U0 + UW, row=k)
+    L = lambda name, k, n=1: R(name, 32 * k, 32 * (k + n))
+    Z = lambda k: R("zz", 512 * k, 512 * k + 512)
+
+    dma("s", R("xw0", 0, V), hbm(T.x[:]), 5.0)
+    dma("a", R("si"), hbm(T.shw[:]))
+    dma("a", R("hi"), hbm(T.hang[:]))
+    dma("a", R("ki"), hbm(T.kid[:]))
+    dma("a", R("bi", 0, 2), hbm(T.bar[:]))
+    dma("s", R("xa"), hbm(T.x[:, 0:2048]), 6.0)
+    iota(R("pi", 0, 1), [[0, 1]], 0, 1)
+    iota(R("ia"), [[1, SG]], 0, 0)
+    iota(R("ic"), [[16, 8], [0, 16]], 0, 0)
+    iota(R("ib"), [[0, 12], [1, 16]], 0, 0)
+    iota(R("jc"), [[7, 512]], W + 6, 0)
+    fill(R("at"), 0.0)
+    fill(R("zero"), 0.0)
+    ts(R("pi", 1, 2), R("pi", 0, 1), 15, A.bitwise_and)
+    cp(R("pc", 0, 2), R("pi", 0, 2))
+    tt(col(2), col(0), col(1), A.subtract)
+    ts(col(3), col(2), 15.0, A.add)
+    cp(R("shn"), R("si"))
+    ts(R("ew"), R("ia", 0, 144), col(3), A.is_equal)
+    ts(R("idn"), R("ia", 0, 128), col(0), A.is_equal)
+    ts(R("oh"), R("ia", 0, 16), col(1), A.is_equal)
+    ts(R("bo"), R("ic"), col(2), A.is_equal)
+    ts(R("tri"), R("ia", 0, 128), col(0), A.is_gt)
+    tt(R("tri"), R("tri"), R("bo"), A.mult)
+
+    def wcol(k, terms):
+        ts(col(k), oh(terms[0][0]), terms[0][1], A.mult)
+        for (r, w) in terms[1:]:
+            ts(col(k), oh(r), w, A.mult, col(k), A.add)
+
+    wcol(8, [(0, 1024.0), (1, 256.0)])
+    wcol(9, [(0, 1.0), (1, 3072.0)])
+    fill(col(30), -0.25)
+    cp(R("hf"), R("hi"))
+    ts(R("pn"), R("hf"), 0.5, A.mult, -0.25, A.add)
+    act(R("wset", 0, 144), R("ew"))
+    act(wb(IDN), R("idn"))
+    act(wb(NID), R("idn"), scale=-1.0)
+    act(wb(ONE), R("bo"))
+    act(wb(NON), R("bo"), scale=-4096.0)
+    cp(R("sh0"), X(R("xw0", 0, V), R("shn")), True)
+    send("sh0", 0, "xw0", V, 1, "sa0")
+    gfill("ut", 0, 6144, 0)
+    dma("g", urow(0), R("zero"), 3.8)
+    dma("g", urow(1), R("zero"), 3.8)
+    gfill("htb", 0, 6144, 0)
+    for n in range(4):
+        node({"g": (2.0, lambda n=n: g.affine_select(T.half[:, 896 * n:896 * n + 896], T.htb[:, 0:896], [[0, 128], [1, 7]],
+                                                     A.is_equal, 0.5, 0, 0))},
+             [R("half", 896 * n, 896 * n + 896)], [R("htb", 0, 896)])
+    gfill("one", 0, 512, 256)
+    gfill("fw", 0, 384, 0)
+    gfill("fw", 896, 1280, 0)
+    act(wb(KV), R("bo"), scale=col(8))
+    act(wb(KW), R("bo"), scale=col(9))
+    ts(R("bf", 0, 2), R("bi", 0, 2), -0.5, A.add)
+    dma("s", R("ft", row=0), R("zero", 0, SG))
+    fill(R("ci", NC, SG), 0)
+    fill(R("ci", SG + NC, 2 * SG), 0)
+    fill(R("fls", NC, SG), 0.0)
+    fill(R("sts", NC, SG), 1.0)
+    ts(R("hk"), R("ki"), float(W), A.is_lt)
+    ts(R("t1", 0, 128), R("idn"), -256.0, A.mult)
+    tt(wb(TRV), R("t1", 0, 128), R("tri"), A.add)
+    ts(R("t2", 0, 128), R("idn"), -4096.0, A.mult)
+    tt(wb(TRU), R("t2", 0, 128), R("tri"), A.add)
+    ts(R("kc"), R("ia", 0, NC), oh(0), A.mult, 1.0, A.add)
+    ts(R("dm"), R("ib"), col(1), A.is_equal)
+    ts(R("hold"), R("ib"), 0.0, A.not_equal)
+    fill(R("cx", 0, 8), 0.0)
+    fill(R("neg"), -1.0)
+    fill(R("zz", 0, 512), 0.0)
+    ts(R("v16"), R("ia"), 16.0, A.mult, col(1), A.add)
+    ts(R("own", 0, SG), R("ia"), float(W // 16 - 1), A.min)
+    ts(R("own", SG, 2 * SG), R("ia"), 0.0, A.mult, col(1), A.add)
+    dma("s", R("at", row=4), R("own", 0, SG))
+    dma("s", R("at", row=5), R("own", SG, 2 * SG))
+    wcol(10, [(0, 1.0), (1, float(SG))])
+    wcol(11, [(4, 16.0), (5, 1.0)])
+    wcol(12, [(2, 0.5), (3, BIG)])
+    wcol(13, [(2, 0.5)])
+    wcol(14, [(0, 16.0), (1, 1.0)])
+    wcol(15, [(0, 1.0 / 1024)])
+    ts(col(16), col(1), float(SG), A.mult)
+    wcol(17, [(0, 1.0 / 32)])
+    ts(col(18), col(1), 2.0, A.mult)
+    for n, k in ((CH, 15), (CM, 16), (ZH, 17), (ZM, 18), (SIG, 10), (NAT, 11), (FL, 12), (FL0, 13), (NP, 14)):
+        act(R("wset", 144 * n, 144 * n + 144), R("ew"), scale=col(k))
+    wcol(19, [(1, 33.0)])
+    ts(R("pc", 24, 30), R("ia", 0, 6), oh(0), A.mult, -1.0, A.mult)
+    ts(R("jc"), R("jc"), oh(0), A.mult, col(19), A.add)
+    ts(R("dum", 0, 32), R("v16", 0, 32), float(U0 + UW), A.add, 0.5, A.mult)
+    ts(R("dum", 32, 64), R("v16", 0, 32), float(U0 + UW), A.add, 0.5, A.mult)
+    ts(R("duf"), R("v16", 0, 32), float(W), A.add)
+    fill(R("lv", 192, 224), 0.0)
+    ts(R("k2"), R("v16", 0, NC), 2.0, A.mult, 1.0, A.add)
+    ts(col(20), col(1), 384.0, A.mult, 192.0, A.add)
+    ts(R("slf"), R("ia", 0, NC), col(20), A.add)
+    ts(R("s2", 0, 24), R("si"), 15, A.bitwise_and)
+    ts(R("s2", 24, 48), R("si"), 4, A.arith_shift_right)
+    ts(R("s3"), R("s2", 0, 24), float(SG), A.mult)
+    tt(R("s3"), R("s3"), R("s2", 24, 48), A.add)
+    cp(R("shs"), R("s3"))
+
+    def sums(cur):
+        for c in range(3):
+            mms(R("b5", 64 * c, 64 * c + 64), wrap(SUM, cur, 1024 * c, 1024 * c + 1024))
+
+    sums("xw0")
+
+    def one_round(r):
+        cur, nxt = xw[r % 2], xw[(r + 1) % 2]
+        last_round = r == RO - 1
+        ab = lambda a, b: R(nxt, W + a, W + b)
+        full = R(cur, 0, W)
+        tt(R("ee", 0, 1024), X(full, R("pn", 0, 64)), R("xa", 0, 1024), A.subtract)
+        act(R("ee", 2048, V), X(full, R("pn", 128, 192)))
+        tt(R("ee", 1024, 2048), X(full, R("pn", 64, 128)), R("xa", 1024, 2048), A.subtract)
+        for h in range(2):
+            mms(R("b%d" % h), [(wb(IDN), R("ee", 2048 + 512 * h, 2560 + 512 * h)), (wb(NID), R(cur, 2048 + 512 * h, 2560 + 512 * h))])
+
+        def gapsum(c):
+            mms(R("b4", 64 * c, 64 * c + 64), wrap(SUM, nxt, W + 1024 * c, W + 1024 * c + 1024))
+
+        act(ab(0, 1024), R("ee", 0, 1024), AF.Abs)
+        gapsum(0)
+        for h in range(2):
+            act(ab(2048 + 512 * h, 2560 + 512 * h), R("b%d" % h), AF.Abs)
+        gapsum(2)
+        act(ab(1024, 2048), R("ee", 1024, 2048), AF.Abs)
+        gapsum(1)
+        if r:
+            cp(R("hf"), R("b3", 0, NC), True)
+            cp(R("hi"), R("b3", 0, NC))
+        ts(R("ci", 0, NC), R("hi"), 5, A.arith_shift_right)
+        ts(R("ci", SG, SG + NC), R("hi"), 1, A.arith_shift_right, 15, A.bitwise_and)
+        ts(R("ci", 2 * SG, 2 * SG + NC), R("hi"), 1, A.bitwise_and)
+        cp(R("ats"), R("ci", 0, 2 * SG))
+        ts(R("b7", 0, NC), R("ci", 2 * SG, 2 * SG + NC), 2.0, A.mult)
+        tt(R("fls", 0, NC), R("b7", 0, NC), R("hk"), A.add)
+        dma("s", R("at", row=0), R("ats", 0, SG))
+        dma("s", R("at", row=1), R("ats", SG, 2 * SG))
+        dma("s", R("at", row=2), R("fls"))
+        ts(R("hv"), R("b5", 0, NC), R("bf", 1, 2), A.is_ge)
+        if r:
+            tt(R("b4", NC, 2 * NC), R("b4", 0, NC), R("flw", 0, NC), A.add)
+        ts(R("cand"), R("b4", NC if r else 0, 2 * NC if r else NC), R("bf", 0, 1), A.is_ge)
+        mms(R("b2", 0, NC), [(wb(ONE), R("cand"))])
+        mms(R("b0", 0, NC), [(wb(NON), R("cand")), (wb(KW), R("kc"))])
+        mms(R("b6", 0, NC), [(wb(TRV), R("cand")), (wb(KV), R("kc"))])
+        mms(R("b3", 0, NC), [(wb(TRU), R("cand"))])
+        act(R("val"), R("b6", 0, NC))
+        scan(R("cx", 1, NC + 1), R("b2", 0, NC), R("zero", 0, NC), 0.0, A.add, A.add)
+        tt(R("b7", 0, NC), R("b0", 0, NC), R("cx", 0, NC), A.max)
+        tt(R("t2"), R("b7", 0, NC), R("dm"), A.mult)
+        scan(R("t3"), R("hold"), R("t2"), 0.0, A.mult, A.add)
+        cp(R("tl"), R("t3", 15, NC, 16))
+        tt(R("t1"), R("b3", 0, NC), R("cx", 0, NC), A.add)
+        ts(R("b3", 0, NC), R("t1"), 512.0 - 4096.0, A.is_lt)
+        tt(R("sts", 0, NC), R("b3", 0, NC), R("hv"), A.max)
+        dma("s", R("at", row=3), R("sts"))
+        cp(X(R("zz"), R("tl")), R("val"))
+        scan(R("b7"), R("neg"), R("zz", 0, 512), 0.0, A.add, A.max)
+        ts(R("hh"), R("b7"), MAGIC1K, A.add, MAGIC1K, A.subtract)
+        mms(R("b1", 0, 32), wrap(CH, "hh", 0, 512), stop=False)
+        tt(R("mt"), R("b7"), R("hh"), A.is_equal)
+        mms(R("b1", 0, 32), wrap(CM, "mt", 0, 512), start=False)
+        ts(L("ng", 0), R("v16", 0, 32), R("cx", NC, NC + 1), A.is_ge, BIG, A.mult)
+        ts(L("sl", 0), R("b1", 0, 32), -1.0, A.add, float(TW - 1), A.min)
+        mms(R("b6"), [(ws(ZH, 1), R("hh")), (ws(ZM, 1), R("mt"))])
+        tt(Z(0), R("b6"), R("jc"), A.add)
+        for n in range(1, 6):
+            act(Z(n), Z(0), bias=col(24 + n))
+        lo, hi = R("b7", 0, NC), R("b7", NC, 2 * NC)
+        ts(lo, R("hf"), float(2 * V), A.is_lt)
+        tt(R("t4"), lo, R("ci", 2 * SG, 2 * SG + NC), A.mult)
+        ts(lo, R("ci", SG, SG + NC), 384.0, A.mult)
+        tt(hi, lo, R("ci", 0, NC), A.add)
+        tt(lo, hi, R("slf"), A.subtract)
+        tt(hi, lo, R("t4"), A.mult)
+        tt(lo, hi, R("slf"), A.add)
+        cp(R("hl"), lo)
+
+        def xgather(k):
+            o = R("ee", 6 - k, 3584, 7, cls=k)
+            w = X(full, L("nl", k))
+            if k == 6:
+                cp(o, w, True)
+            else:
+                lin(o, w, 0.5, col(30))
+
+        def addresses(k, n, hk):
+            t = L("ta", k, n)
+            ts(t, L("sl", k, n), 2.0, A.mult, U0 / 2 + 1.0, A.add)
+            if hk is not None:
+                tt(t, t, hk, A.add)
+            tt(t, t, L("mm", k, n), A.max)
+            tt(t, t, L("lv", k + 1, n), A.subtract)
+            tt(t, t, L("dum", 0, n), A.min)
+            ts(L("al", k, n), t, 2.0, A.mult)
+            for m in range(k, k + n):
+                sput(X(R("ut"), L("al", m)), Z(m), True)
+
+        def hold_on(k, src):
+            t = L("tb", k - 1)
+            tt(t, src, L("nf", k - 1), A.subtract)
+            tt(t, t, L("lv", k - 1), A.mult)
+            tt(L("nf", k), t, L("nf", k - 1), A.add)
+            cp(L("nl", k), L("nf", k))
+
+        def logic(k):
+            bank = "b%d" % (2 + k % 2)
+            tt(L("mm", k), R(bank, 0, 32), L("ng", k), A.max)
+            ts(L("lv", k), L("mm", k), BIG, A.is_lt)
+            if k < 5:
+                ts(L("ng", k + 1), L("mm", k), 1.0, A.is_ge, BIG, A.mult)
+            if 1 <= k <= 4:
+                addresses(k - 1, 1, None if last_round or k == 1 else L("mm", k - 2))
+            if k == 5:
+                addresses(4, 2, None if last_round else L("mm", 3, 2))
+            if k:
+                hold_on(k, R(bank, 32, 64))
+            else:
+                cp(L("nf", 0), R(bank, 32, 64))
+                cp(L("nl", 0), R(bank, 32, 64))
+            xgather(k)
+
+        for k in range(6):
+            gk = "g%d" % (k % 2)
+            p1, bank = R("b%d" % (k % 2), 0, 32), "b%d" % (2 + k % 2)
+            cp(R(gk), X(R("at"), L("sl", k)), True)
+            if k < 5:
+                mms(p1, wrap(SIG, gk, 0, 512))
+            mms(R(bank, 0, 32), wrap(FL if k else FL0, gk, 0, 512))
+            mms(R(bank, 32, 64), wrap(NAT, gk, 0, 512))
+            if k == 5:
+                mms(p1, wrap(NP, gk, 0, 512))
+            if k:
+                logic(k - 1)
+            if k < 5:
+                cp(L("sl", k + 1), p1)
+        logic(5)
+        hold_on(6, R("b1", 0, 32))
+        xgather(6)
+        dma("s", R("wrp"), urow(0), 3.8)
+        dma("s", R("wrd"), urow(1), 3.8)
+        if not last_round:
+            t = R("td")
+            ts(t, L("nf", 6), float(V), A.is_lt, BIG, A.mult)
+            tt(t, t, L("nf", 6), A.add)
+            tt(t, t, L("ng", 0), A.add)
+            tt(t, t, R("duf"), A.min)
+            ts(R("fa"), t, -float(V), A.add)
+            sput(X(R("fw", 896 * r, 896 * r + 896), R("fa")), R("one"))
+            send("fw", 896 * r, "fl%d" % r, 0, -1, "fa%d" % r)
+            gfill("zz", 0, 512, 0)
+            tt(R("tc"), L("lv", 0, 6), L("lv", 1, 6), A.subtract)
+            tt(R("tc"), R("tc"), R("mm"), A.mult)
+            tt(L("tc", 0, 3), L("tc", 0, 3), L("tc", 3, 3), A.add)
+            tt(L("tc", 0), L("tc", 0), L("tc", 1), A.add)
+            tt(L("tc", 0), L("tc", 0), L("tc", 2), A.add)
+            ts(L("tc", 1), L("tc", 0), 1.0, A.is_ge)
+            tt(L("tc", 0), L("tc", 1), L("tc", 0), A.subtract)
+            ts(L("tc", 0), L("tc", 0), 0.5, A.add, 2 * BIG, A.mult)
+            ts(L("tc", 3), L("sl", 0), 0.5, A.mult, U0 / 2, A.add)
+            tt(L("tc", 0), L("tc", 0), L("tc", 3), A.add)
+            tt(L("tc", 0), L("tc", 0), L("dum", 0), A.min)
+            ts(R("a0"), L("tc", 0), 2.0, A.mult)
+            if r:
+                dma("s", R("ut", U0, U0 + TW, row=2), R("zero", 0, SG))
+            sput(X(R("ut"), R("a0")), R("one"))
+            dma("s", R("h0"), R("ut", U0, U0 + TW, row=2))
+            dma("s", urow(0), R("zero"), 3.8)
+            dma("s", urow(1), R("zero"), 3.8)
+        scan(R("uh"), R("half"), R("ee"), 0.0, A.mult, A.add)
+        ts(R(cur, W, XWID), R("uh"), MAGIC, A.add, MAGIC, A.subtract)
+        tt(R("b7", 0, 384), R("wrp", 0, 768, 2), R("wrp", 1, 768, 2), A.max)
+        cp(R("t3"), R("b7", 1, 384, 2), True)
+        tt(R("b6", 0, NC), R("b7", 0, 384, 2), R("t3"), A.max)
+        tt(R("b6", NC, 2 * NC), R("b6", 0, NC), R("v16", 0, NC), A.max)
+        cp(R("xl"), R("b6", NC, 2 * NC))
+        for h in range(6):
+            cp(R(nxt, 512 * h, 512 * h + 512), X(R(cur), R("xl", 32 * h, 32 * h + 32)), True)
+        if last_round:
+            for h in range(2):
+                dma("s", hbm(T.y[:, 1536 * h:1536 * h + 1536]), R(nxt, 1536 * h, 1536 * h + 1536), 3.5)
+        else:
+            cp(R("sh%d" % (r + 1)), X(R(nxt, 0, V), R("shn")), True)
+            send("sh%d" % (r + 1), 0, nxt, V, 1, "sa%d" % (r + 1))
+            sums(nxt)
+        lo, hi = R("b4", 0, NC), R("b4", NC, 2 * NC)
+        ts(hi, R("b7", 0, 384, 2), 0.0, A.is_gt)
+        tt(R("t1"), R("wrd", 2, 768, 4), R("wrd", 3, 768, 4), A.max)
+        tt(lo, hi, R("hk"), A.mult)
+        tt(R("hs", NC, 2 * NC), lo, R("hf"), A.add)
+        tt(R("t2"), hi, R("hf"), A.mult)
+        ts(lo, R("t1"), MAGIC, A.add, MAGIC + 64.0, A.subtract)
+        tt(R("t2"), lo, R("t2"), A.max)
+        ts(lo, R("b6", 0, NC), 0.0, A.is_equal)
+        tt(hi, lo, R("k2"), A.mult)
+        tt(R("hs", 0, NC), hi, R("t2"), A.max)
+        if last_round:
+            tab = R("ut", 0, 6144)
+            dma("s", R("ut", 0, 6144, row=0), R("hs"))
+            for h in range(6):
+                cp(R("ut", 6144 + 512 * h, 6656 + 512 * h), X(tab, R("hl", 32 * h, 32 * h + 32)), True)
+            dma("s", hbm(T.yh[:]), R("ut", 6144, 6144 + V, row=0))
+            return
+        cp(R("hsh"), R("hs"), True)
+        dma("s", R("htb", row=0), R("hsh"))
+        tt(R("hsl"), R("hs"), R("hsh"), A.subtract)
+        dma("s", R("htb", row=1), R("hsl"))
+        dma("s", R("xa"), R(nxt, 0, 2048), 4.0)
+        for c in range(3):
+            for h in (2 * c, 2 * c + 1):
+                cp(ab(512 * h, 512 * h + 512), X(R("htb"), R("hl", 32 * h, 32 * h + 32)), True)
+            mms(R("b3", 64 * c, 64 * c + 64), wrap(SUM, nxt, W + 1024 * c, W + 1024 * c + 1024))
+        lo, hi = R("b7", 0, NC), R("b7", NC, 2 * NC)
+        ts(lo, R("b6", 0, NC), 0.0, A.is_equal)
+        tt(R("t5"), lo, R("hk"), A.mult)
+        tt(R("t6"), R("wrp", 1, 768, 4), R("wrp", 3, 768, 4), A.max)
+        tt(lo, R("t6"), R("t5"), A.max)
+        tt(hi, lo, R("h0", 0, NC), A.max)
+        ts(R("hk"), hi, 0.5, A.is_gt)
+        sput(X(R("ft"), R("shs")), R("fl%d" % r))
+        dma("s", R("flw"), R("ft", row=0))
+        ts(R("pn"), R("b3", 0, NC), 0.5, A.mult, -0.25, A.add)
+
+    for r in range(RO):
+        one_round(r)
+    emit()

@@ -2,17 +2,18 @@ import numpy as np
 from concourse.bass import DstId, RemoteDMATransfer
 from concourse.mybir import AluOpType, ActivationFunctionType
 
-V, W, NC, SG, RO = 3072, 3456, 192, 224, 3
+V, W, NC, SG, RO = 3072, 3456, 192, 216, 3
+S2 = 2 * SG
 XWID = W + 3584
-TW = 16 * SG
-U0 = 8
-UW = 4 * TW
-BIG = 32768.0
+PTW = 16 * S2
+ROFF = PTW + 24
+ATW = ROFF + V + 8
+ZW = 3264
+BIG = 8192.0
 MAGIC = 12582912.0
-MAGIC1K = MAGIC * 1024.0
 CYC, PEC, GATH, SCAT, WAKE = 1.04e-3, 0.6e-3, 1.56, 3.8, 0.06
 MODELS = (((0.7, 0.45, 0.75, 1.0), 0.88), ((1.0, 1.0, 1.0, 1.0), 1.0), ((1.3, 1.55, 1.6, 1.0), 1.25))
-TRIES = 2500
+TRIES = 1500
 PLAN = {}
 
 F, B, I, U, H = "float32", "bfloat16", "int32", "uint16", "float16"
@@ -23,31 +24,30 @@ def _s(n, d):
 
 
 SCRATCH = {
-    "xw0": _s(XWID, B), "xw1": _s(XWID, B), "at": _s(TW, B), "ut": _s(U0 + UW + 512, F), "htb": _s(6144, B),
-    "xa": _s(2048, B), "ee": _s(3584, B), "uh": _s(3584, H), "half": _s(3584, B), "ft": _s(TW, F),
-    "wrp": _s(4 * SG, F), "wrd": _s(4 * SG, F), "zero": _s(4 * SG, F),
-    "g0": _s(512, B), "g1": _s(512, B), "zz": _s(3328, F), "jc": _s(512, F), "neg": _s(512, B),
-    "hh": _s(512, B), "mt": _s(512, B), "one": _s(512, F),
-    "sh0": _s(384, B), "sh1": _s(384, B), "sh2": _s(384, B), "fw": _s(1792, F),
-    "fl0": _s(384, F), "fl1": _s(384, F), "flw": _s(SG, F), "h0": _s(SG, F),
-    "hi": _s(NC, I), "ki": _s(NC, I), "si": _s(24, I), "s2": _s(48, I), "s3": _s(24, F), "bi": _s(8, I), "bf": _s(8, F),
-    "shn": _s(24, U), "shs": _s(24, U), "pn": _s(NC, U), "hl": _s(NC, U), "xl": _s(NC, U), "tl": _s(12, U),
-    "ci": _s(3 * SG, I), "ats": _s(2 * SG, B), "fls": _s(SG, B), "sts": _s(SG, B), "own": _s(2 * SG, B),
-    "hf": _s(NC, F), "hk": _s(NC, F), "hv": _s(NC, F), "t1": _s(NC, F), "t2": _s(NC, F), "t3": _s(NC, F),
-    "t4": _s(NC, F), "t5": _s(NC, F), "t6": _s(NC, F),
-    "hs": _s(384, F), "hsh": _s(384, B), "hsl": _s(384, B),
-    "cand": _s(NC, B), "cx": _s(200, F), "val": _s(NC, F), "kc": _s(NC, B),
-    "pi": _s(8, I), "pc": _s(32, F), "oh": _s(16, F), "ia": _s(SG, F), "ib": _s(NC, F), "ic": _s(128, F),
-    "v16": _s(SG, F), "k2": _s(NC, F), "slf": _s(NC, F), "dm": _s(NC, F), "hold": _s(NC, F),
-    "ew": _s(144, F), "wset": _s(144 * 10, B), "bo": _s(128, F), "tri": _s(128, F), "idn": _s(128, F),
-    "wblk": _s(128 * 8, B),
-    "sl": _s(192, U), "nl": _s(224, U), "al": _s(192, U), "fa": _s(32, U), "a0": _s(32, U),
-    "mm": _s(192, F), "lv": _s(224, F), "ng": _s(192, F), "nf": _s(224, F),
-    "ta": _s(192, F), "tb": _s(192, F), "tc": _s(192, F), "td": _s(32, F), "dum": _s(64, F), "duf": _s(32, F),
+    "xw0": _s(XWID, B), "xw1": _s(XWID, B), "xw2": _s(XWID, B), "at": _s(ATW, B), "pt": _s(PTW + 512, F),
+    "ee": _s(3584, B), "uh": _s(3584, H), "half": _s(896, B), "dd": _s(V, B), "gk": _s(V, B), "src": _s(2048, F),
+    "z1": _s(ZW + 1024, B), "z2": _s(ZW + 1024, F), "ft": _s(V, F), "fw": _s(1792, F), "one": _s(512, F),
+    "fl0": _s(384, F), "fl1": _s(384, F), "flw": _s(NC, F), "thr": _s(NC, F),
+    "sh0": _s(384, B), "sh1": _s(384, B), "sh2": _s(384, B), "sg": _s(384, B),
+    "po0": _s(S2, F), "po1": _s(S2, F), "po2": _s(S2, F), "pbg": _s(S2, F),
+    "jc": _s(512, B), "jt": _s(1024, B), "s1": _s(512, B), "s2": _s(512, B), "mt": _s(512, B), "neg": _s(512, B), "pos": _s(512, B),
+    "zero": _s(1024, B), "xa": _s(2048, B),
+    "hi": _s(NC, I), "ki": _s(NC, I), "ci": _s(3 * NC, I), "hm": _s(NC, I), "si": _s(24, I), "sj": _s(48, I), "sf": _s(72, F),
+    "bi": _s(8, I), "bf": _s(8, F), "shn": _s(24, U), "shs": _s(24, U), "shp": _s(24, U), "shl": _s(24, U),
+    "pn": _s(NC, U), "pl": _s(NC, U), "xl": _s(NC, U), "tl": _s(12, U), "l1": _s(12, U), "l2": _s(12, U),
+    "da": _s(NC, B), "de": _s(NC, B), "hk": _s(NC, B), "hv": _s(NC, B), "val": _s(NC, B), "cz": _s(NC, F),
+    "sda": _s(S2, B), "sde": _s(S2, B), "shk": _s(S2, B), "sns": _s(S2, B), "oc": _s(S2, B), "oe": _s(S2, B),
+    "aa": _s(NC, F), "thk": _s(NC, F), "cc": _s(400, B), "kb": _s(32, B), "tu": _s(32, F),
+    "y1": _s(NC, F), "y2": _s(NC, F), "y3": _s(NC, F),
+    "pi": _s(8, I), "pc": _s(48, F), "bt": _s(8, F), "oh": _s(16, F), "ia": _s(SG, F), "ic": _s(128, F), "v16": _s(SG, F),
+    "ew": _s(144, F), "wset": _s(144 * 11, B), "bo": _s(128, F), "tri": _s(128, F), "idn": _s(128, F), "tmp": _s(256, F),
+    "wblk": _s(128 * 8, B), "st": _s(128 * 10, B),
+    "sl": _s(192, U), "nl": _s(224, U), "al": _s(192, U), "fa": _s(32, U),
+    "ta": _s(192, F), "td": _s(32, F), "dum": _s(64, F), "duf": _s(32, F), "lt": _s(24, F),
 }
 for _k in range(8):
     SCRATCH["b%d" % _k] = ("psum", [128, 512], F)
-NDMA = 60
+NDMA = 70
 SEMAPHORES = ["cv", "ca", "cp", "cg", "sent", "sa0", "sa1", "sa2", "fa0", "fa1"] + ["d%d" % _k for _k in range(NDMA)]
 
 
@@ -136,6 +136,10 @@ def rank_program(g, core, T, topo):
         node({"v": (vcost(out, [in_], half(out, in_)), lambda: g.vector.tensor_scalar(out[0], in_[0], ap(scale), ap(bias), A.mult, A.add)),
               "a": aopt(out, in_, AF.Identity, bias, scale)}, [out], [in_, scale, bias])
 
+    def relu(out, in_, bias):
+        node({"v": (vcost(out, [in_], 1.0), lambda: g.vector.tensor_scalar(out[0], in_[0], bias[0], 0.0, A.add, A.max)),
+              "a": aopt(out, in_, AF.Relu, bias, 1.0)}, [out], [in_, bias])
+
     def tt(out, a, b, op):
         node({"v": (vcost(out, [a], 1.0 if a[5] or b[5] else 2.0), lambda: g.vector.tensor_tensor(out[0], a[0], b[0], op))}, [out], [a, b])
 
@@ -147,8 +151,8 @@ def rank_program(g, core, T, topo):
             node({"v": (c, lambda: g.vector.tensor_scalar(out[0], a[0], ap(s1), ap(s2), op0, op1))}, [out], [a, s1, s2])
 
     def scan(out, d0, d1, init, op0, op1):
-        node({"v": (vcost(out, [], half(out, d0, d1)), lambda: g.vector.tensor_tensor_scan(out[0], d0[0], d1[0], init, op0, op1))},
-             [out], [d0, d1])
+        node({"v": (vcost(out, [], half(out, d0, d1)), lambda: g.vector.tensor_tensor_scan(out[0], d0[0], d1[0], ap(init), op0, op1))},
+             [out], [d0, d1, init])
 
     def fill(out, c):
         node({"v": (vcost(out, [], half(out)), lambda: g.vector.memset(out[0], c))}, [out], [])
@@ -156,23 +160,30 @@ def rank_program(g, core, T, topo):
     def act(out, in_, func=None, bias=0.0, scale=1.0):
         node({"a": aopt(out, in_, AF.Identity if func is None else func, bias, scale)}, [out], [in_, bias, scale])
 
-    def sput(o, z, either=False):
-        opts = {"a": (vcost(o, [z], 1.0), lambda: g.scalar.activation(o[0], z[0], AF.Silu))}
-        if either:
-            opts["v"] = (vcost(o, [z], 1.0), lambda: g.vector.tensor_copy(o[0], z[0]))
-        node(opts, [o], [z])
+    def sput(o, z):
+        node({"a": (vcost(o, [z], 1.0), lambda: g.scalar.activation(o[0], z[0], AF.Silu)),
+              "v": (vcost(o, [z], 1.0), lambda: g.vector.tensor_copy(o[0], z[0]))}, [o], [z])
 
-    def iota(out, pattern, base, mult):
+    def iopt(out, pattern, base, mult):
         c = 0.13 + 2 * out[3] * CYC
         if SCRATCH[out[1][0][0]][2] == I:
-            node({"g": (c, lambda: g.iota(out[0], pattern, base, mult))}, [out], [])
-        else:
-            node({"g": (c, lambda: g.iota(out[0], pattern, base, mult, allow_small_or_imprecise_dtypes=True))}, [out], [])
+            return (c, lambda: g.iota(out[0], pattern, base, mult))
+        return (c, lambda: g.iota(out[0], pattern, base, mult, allow_small_or_imprecise_dtypes=True))
 
-    def gfill(name, a, b, c):
-        for lo in range(a, b, 1024):
-            hi = min(b, lo + 1024)
-            iota(R(name, lo, hi), [[0, hi - lo]], c, 0)
+    def iota(out, pattern, base, mult):
+        node({"g": iopt(out, pattern, base, mult)}, [out], [])
+
+    def wipe(name, a, b, c, qs="gv", step=512):
+        for lo in range(a, b, step):
+            o = R(name, lo, min(b, lo + step))
+            opts = {}
+            if "g" in qs:
+                opts["g"] = iopt(o, [[0, o[3]]], c, 0)
+            if "v" in qs:
+                opts["v"] = (vcost(o, [], half(o)), lambda o=o: g.vector.memset(o[0], float(c)))
+            if "a" in qs:
+                opts["a"] = aopt(o, R("zero", 0, o[3]), AF.Identity, 0.0, 1.0)
+            node(opts, [o], [R("zero", 0, o[3])] if "a" in qs else [])
 
     def mms(out, pairs, start=True, stop=True):
         def make():
@@ -303,36 +314,39 @@ def rank_program(g, core, T, topo):
     def wb(n):
         return R("wblk", 128 * n, 128 * n + 128)
 
+    def st(n):
+        return R("st", 128 * n, 128 * n + 128)
+
     def wrap(n, name, a, b):
         return [(ws(n, i), R(name, a + i, b, 16)) for i in range(16)]
 
-    SUM, SIG, NAT, FL, FL0, NP, CH, CM, ZH, ZM = range(10)
-    IDN, NID, TRV, TRU, ONE, NON, KV, KW = range(8)
-    xw = ["xw0", "xw1"]
+    SUM, NEG, TWO, NXT, NTN, NTO, UW, CH, CM, WW, SW = range(11)
+    IDN, NID, I216, TRV, TRU, ONE, HVY = range(7)
+    MF, MFP, MF0, MN, MN1, MP, Y2 = range(7)
+    xw = ["xw0", "xw1", "xw2", "xw0"]
     col = lambda k: R("pc", k, k + 1)
     oh = lambda k: R("oh", k, k + 1)
-    urow = lambda k: R("ut", U0, U0 + UW, row=k)
     L = lambda name, k, n=1: R(name, 32 * k, 32 * (k + n))
-    Z = lambda k: R("zz", 512 * k, 512 * k + 512)
+    G = lambda k, n=1: R("gk", 512 * k, 512 * (k + n))
+    odd = lambda name: R(name, SG, SG + NC)
 
+    dma("s", R("si"), hbm(T.shw[:]))
     dma("s", R("xw0", 0, V), hbm(T.x[:]), 5.0)
-    dma("a", R("si"), hbm(T.shw[:]))
     dma("a", R("hi"), hbm(T.hang[:]))
     dma("a", R("ki"), hbm(T.kid[:]))
     dma("a", R("bi", 0, 2), hbm(T.bar[:]))
-    dma("s", R("xa"), hbm(T.x[:, 0:2048]), 6.0)
+    dma("s", R("xa"), hbm(T.x[:, 0:2048]), 7.0)
     iota(R("pi", 0, 1), [[0, 1]], 0, 1)
     iota(R("ia"), [[1, SG]], 0, 0)
     iota(R("ic"), [[16, 8], [0, 16]], 0, 0)
-    iota(R("ib"), [[0, 12], [1, 16]], 0, 0)
-    iota(R("jc"), [[7, 512]], W + 6, 0)
-    fill(R("at"), 0.0)
     fill(R("zero"), 0.0)
     ts(R("pi", 1, 2), R("pi", 0, 1), 15, A.bitwise_and)
     cp(R("pc", 0, 2), R("pi", 0, 2))
     tt(col(2), col(0), col(1), A.subtract)
     ts(col(3), col(2), 15.0, A.add)
     cp(R("shn"), R("si"))
+    cp(R("sh0"), X(R("xw0", 0, V), R("shn")), True)
+    send("sh0", 0, "xw0", V, 1, "sa0")
     ts(R("ew"), R("ia", 0, 144), col(3), A.is_equal)
     ts(R("idn"), R("ia", 0, 128), col(0), A.is_equal)
     ts(R("oh"), R("ia", 0, 16), col(1), A.is_equal)
@@ -341,162 +355,202 @@ def rank_program(g, core, T, topo):
     tt(R("tri"), R("tri"), R("bo"), A.mult)
 
     def wcol(k, terms):
-        ts(col(k), oh(terms[0][0]), terms[0][1], A.mult)
+        lin(col(k), oh(terms[0][0]), terms[0][1], 0.0)
         for (r, w) in terms[1:]:
-            ts(col(k), oh(r), w, A.mult, col(k), A.add)
+            lin(col(k), oh(r), w, col(k))
 
-    wcol(8, [(0, 1024.0), (1, 256.0)])
-    wcol(9, [(0, 1.0), (1, 3072.0)])
-    fill(col(30), -0.25)
-    cp(R("hf"), R("hi"))
-    ts(R("pn"), R("hf"), 0.5, A.mult, -0.25, A.add)
-    act(R("wset", 0, 144), R("ew"))
-    act(wb(IDN), R("idn"))
-    act(wb(NID), R("idn"), scale=-1.0)
-    act(wb(ONE), R("bo"))
-    act(wb(NON), R("bo"), scale=-4096.0)
-    cp(R("sh0"), X(R("xw0", 0, V), R("shn")), True)
-    send("sh0", 0, "xw0", V, 1, "sa0")
-    gfill("ut", 0, 6144, 0)
-    dma("g", urow(0), R("zero"), 3.8)
-    dma("g", urow(1), R("zero"), 3.8)
-    gfill("htb", 0, 6144, 0)
-    for n in range(4):
-        node({"g": (2.0, lambda n=n: g.affine_select(T.half[:, 896 * n:896 * n + 896], T.htb[:, 0:896], [[0, 128], [1, 7]],
-                                                     A.is_equal, 0.5, 0, 0))},
-             [R("half", 896 * n, 896 * n + 896)], [R("htb", 0, 896)])
-    gfill("one", 0, 512, 256)
-    gfill("fw", 0, 384, 0)
-    gfill("fw", 896, 1280, 0)
-    act(wb(KV), R("bo"), scale=col(8))
-    act(wb(KW), R("bo"), scale=col(9))
-    ts(R("bf", 0, 2), R("bi", 0, 2), -0.5, A.add)
-    dma("s", R("ft", row=0), R("zero", 0, SG))
-    fill(R("ci", NC, SG), 0)
-    fill(R("ci", SG + NC, 2 * SG), 0)
-    fill(R("fls", NC, SG), 0.0)
-    fill(R("sts", NC, SG), 1.0)
-    ts(R("hk"), R("ki"), float(W), A.is_lt)
-    ts(R("t1", 0, 128), R("idn"), -256.0, A.mult)
-    tt(wb(TRV), R("t1", 0, 128), R("tri"), A.add)
-    ts(R("t2", 0, 128), R("idn"), -4096.0, A.mult)
-    tt(wb(TRU), R("t2", 0, 128), R("tri"), A.add)
-    ts(R("kc"), R("ia", 0, NC), oh(0), A.mult, 1.0, A.add)
-    ts(R("dm"), R("ib"), col(1), A.is_equal)
-    ts(R("hold"), R("ib"), 0.0, A.not_equal)
-    fill(R("cx", 0, 8), 0.0)
+    def wset(n, scale):
+        lin(R("wset", 144 * n, 144 * n + 144), R("ew"), scale, 0.0)
+
+    fill(col(4), -0.25)
+    fill(col(5), -17.0)
+    fill(col(6), -32.0)
+    fill(col(7), 40.0)
+    ts(col(8), col(1), 2.0, A.mult, 1.0, A.add)
+    ts(col(9), col(1), float(S2), A.mult, float(SG), A.add)
+    ts(col(10), col(1), 12.0, A.mult, float(V), A.add)
+    ts(col(11), col(1), float(NC), A.mult, float(ROFF - SG), A.add)
+    ts(col(12), col(1), 6.0, A.mult)
+    wset(SUM, 1.0)
+    wset(NEG, -1.0)
+    wset(TWO, 2.0)
+    wset(CM, col(11))
+    lin(wb(IDN), R("idn"), 1.0, 0.0)
+    lin(wb(NID), R("idn"), -1.0, 0.0)
+    lin(wb(I216), R("idn"), float(SG), 0.0)
+    lin(wb(HVY), R("idn"), -4096.0, 0.0)
+    lin(wb(ONE), R("bo"), 1.0, 0.0)
+    lin(R("tmp", 0, 128), R("idn"), 17.0, 0.0)
+    tt(wb(TRV), R("tmp", 0, 128), R("tri"), A.add)
+    lin(R("tmp", 128, 256), R("idn"), -4096.0, 0.0)
+    tt(wb(TRU), R("tmp", 128, 256), R("tri"), A.add)
+    for n, terms in ((NXT, [(0, 1.0), (4, 1.0), (1, float(SG)), (5, float(SG))]), (NTO, [(4, 16.0), (5, 0.5)]),
+                     (UW, [(4, 1.0), (5, float(SG)), (3, -BIG)]), (CH, [(0, 1.0 / 32)]),
+                     (WW, [(3, 1.0), (5, 1.0), (4, 1.0 / 32), (6, 1.0 / 32), (11, 1.0 / 32), (10, BIG / 32)]),
+                     (SW, [(7, 7.0), (8, 7.0 / 32), (9, 1.0 / 32)])):
+        wcol(16 + n, terms)
+        wset(n, col(16 + n))
+    lin(col(16 + NTN), oh(0), 16.0, col(16 + NTO))
+    lin(col(16 + NTN), oh(1), 0.5, col(16 + NTN))
+    wset(NTN, col(16 + NTN))
+    wipe("st", 0, 1280, 0, "va")
+
+    def scol(n, r, c, w=1.0):
+        ts(R("st", 128 * n + r, 128 * n + 128, 16, cls=r), R("bo", 0, 128, 16), c, A.mult, w, A.mult)
+
+    wcol(30, [(6, 224.0), (7, 7.0)])
+    wcol(31, [(4, 32.0), (3, BIG)])
+    wcol(32, [(5, 32.0), (3, BIG)])
+    wcol(33, [(2, 128.0), (3, -32.0)])
+    for r, c, w in ((0, col(30), 1.0), (5, oh(4), 32.0), (6, oh(5), 32.0), (7, oh(6), 32.0), (8, oh(7), 32.0)):
+        scol(MF, r, c, w)
+    for r, c, w in ((2, oh(3), 16.0), (11, oh(3), -16.0), (5, oh(3), -BIG), (6, oh(3), -BIG), (3, col(31), 1.0), (4, col(32), 1.0)):
+        scol(MN, r, c, w)
+    cp(st(MFP), st(MF), True)
+    cp(st(MF0), st(MF), True)
+    cp(st(MN1), st(MN), True)
+    scol(MFP, 1, oh(2), 64.0)
+    scol(MP, 1, oh(2), 64.0)
+    for k, n in enumerate((MF0, MN1, Y2, Y2 + 1, Y2 + 2, Y2 + 3)):
+        scol(n, 1, col(33), float(2 ** k))
+    wcol(34, [(0, W + 6.0), (1, 32.0), (2, 16.0), (3, -BIG), (4, -BIG - 32), (5, -BIG), (6, -BIG - 32), (7, 480.0), (8, 416.0),
+              (9, 352.0), (10, 32.0), (11, 16.0)])
+    wcol(35, [(0, -1.0), (9, -32.0)])
+    lin(R("bt", 0, 6), R("ia", 0, 6), col(35), col(34))
+    lin(R("bt", 6, 7), oh(1), -2016.0, R("bt", 0, 1))
+    for r, w in ((2, -16.0), (5, BIG), (6, BIG), (11, 16.0)):
+        lin(R("bt", 5, 6), oh(r), w, R("bt", 5, 6))
+    lin(col(36), oh(1), 32.0, 0.0)
+
+    wipe("at", 0, ATW, 0, "gva", 1024)
+    wipe("pt", 0, PTW, 0, "gva")
+    for r in range(RO):
+        wipe("z1", 512 * r, 512 * r + 512, -1, "v")
+        wipe("z2", 512 * r, 512 * r + 512, 32)
+    wipe("ft", 0, V, 0, "gva")
+    wipe("one", 0, 512, 256)
+    wipe("fw", 0, 384, 0, "gva")
+    wipe("fw", 896, 1280, 0, "gva")
+    fill(R("half"), 0.5)
+    fill(R("half", 0, 896, 7), 0.0)
     fill(R("neg"), -1.0)
-    fill(R("zz", 0, 512), 0.0)
-    ts(R("v16"), R("ia"), 16.0, A.mult, col(1), A.add)
-    ts(R("own", 0, SG), R("ia"), float(W // 16 - 1), A.min)
-    ts(R("own", SG, 2 * SG), R("ia"), 0.0, A.mult, col(1), A.add)
-    dma("s", R("at", row=4), R("own", 0, SG))
-    dma("s", R("at", row=5), R("own", SG, 2 * SG))
-    wcol(10, [(0, 1.0), (1, float(SG))])
-    wcol(11, [(4, 16.0), (5, 1.0)])
-    wcol(12, [(2, 0.5), (3, BIG)])
-    wcol(13, [(2, 0.5)])
-    wcol(14, [(0, 16.0), (1, 1.0)])
-    wcol(15, [(0, 1.0 / 1024)])
-    ts(col(16), col(1), float(SG), A.mult)
-    wcol(17, [(0, 1.0 / 32)])
-    ts(col(18), col(1), 2.0, A.mult)
-    for n, k in ((CH, 15), (CM, 16), (ZH, 17), (ZM, 18), (SIG, 10), (NAT, 11), (FL, 12), (FL0, 13), (NP, 14)):
-        act(R("wset", 144 * n, 144 * n + 144), R("ew"), scale=col(k))
-    wcol(19, [(1, 33.0)])
-    ts(R("pc", 24, 30), R("ia", 0, 6), oh(0), A.mult, -1.0, A.mult)
-    ts(R("jc"), R("jc"), oh(0), A.mult, col(19), A.add)
-    ts(R("dum", 0, 32), R("v16", 0, 32), float(U0 + UW), A.add, 0.5, A.mult)
-    ts(R("dum", 32, 64), R("v16", 0, 32), float(U0 + UW), A.add, 0.5, A.mult)
+    fill(R("pos"), 1.0)
+    fill(R("jc"), 0.0)
+    iota(R("jt", 0, 512), [[1, 16], [0, 32]], 0, 0)
+    iota(R("jt", 512, 1024), [[0, 16], [1, 32]], 0, 0)
+    dma("s", R("jc", row=6), R("jt", 0, 512, row=6))
+    dma("s", R("jc", row=7), R("jt", 512, 1024, row=7))
+    for name, c in (("sda", 0.0), ("sde", 0.0), ("shk", 0.0), ("sns", -1.0)):
+        fill(R(name, NC, S2), c)
+    lin(R("v16"), R("ia"), 16.0, col(1))
+    fill(R("pbg", 0, SG), 0.0)
+    cp(R("pbg", SG, S2), R("v16"), True)
+    for h in range(2):
+        cp(R("oc", SG * h, SG * h + SG), R("ia"), True)
+        lin(R("oe", SG * h, SG * h + SG), R("ia"), 0.0, col(8))
+    dma("s", R("at", 0, PTW, row=4), R("oc"))
+    dma("s", R("at", 0, PTW, row=5), R("oe"))
+    dma("s", R("at", ROFF, ROFF + V, row=4), R("oc", 0, NC))
+    dma("s", R("at", ROFF, ROFF + V, row=5), R("oe", 0, NC))
+    dma("s", R("at", ROFF, ROFF + V, row=3), R("pos", 0, NC))
+    fill(R("cc", 0, 16), 0.0)
+    fill(R("cc", NC, NC + 16), 0.0)
+    fill(R("kb", 0, 13), 0.0)
+    lin(R("kb", 13, 25), R("ia", 0, 12), -1.0 / 4096, 0.0)
+    ts(R("cz"), R("ia", 0, NC), 1.0, A.add, 32.0, A.mult)
+    for h in range(2):
+        ts(L("dum", h), R("v16", 0, 32), PTW - BIG, A.add)
     ts(R("duf"), R("v16", 0, 32), float(W), A.add)
-    fill(R("lv", 192, 224), 0.0)
-    ts(R("k2"), R("v16", 0, NC), 2.0, A.mult, 1.0, A.add)
-    ts(col(20), col(1), 384.0, A.mult, 192.0, A.add)
-    ts(R("slf"), R("ia", 0, NC), col(20), A.add)
-    ts(R("s2", 0, 24), R("si"), 15, A.bitwise_and)
-    ts(R("s2", 24, 48), R("si"), 4, A.arith_shift_right)
-    ts(R("s3"), R("s2", 0, 24), float(SG), A.mult)
-    tt(R("s3"), R("s3"), R("s2", 24, 48), A.add)
-    cp(R("shs"), R("s3"))
+    ts(R("bf", 0, 1), R("bi", 0, 1), -0.5, A.add)
+    ts(R("bf", 1, 2), R("bi", 1, 2), -1.0, A.mult, 0.5, A.add)
+    ts(R("hk"), R("ki"), float(W), A.is_lt)
+    ts(R("sj", 0, 24), R("si"), 15, A.bitwise_and)
+    ts(R("sj", 24, 48), R("si"), 4, A.arith_shift_right)
+    cp(R("sf", 48, 72), R("si"))
+    ts(R("sf", 0, 24), R("sj", 0, 24), float(NC), A.mult)
+    ts(R("sf", 24, 48), R("sj", 0, 24), float(S2), A.mult, float(SG), A.add)
+    tt(R("sf", 0, 24), R("sf", 0, 24), R("sj", 24, 48), A.add)
+    tt(R("sf", 24, 48), R("sf", 24, 48), R("sj", 24, 48), A.add)
+    cp(R("shs"), R("sf", 0, 24))
+    cp(R("shp"), R("sf", 24, 48))
+    iota(R("lt", 0, 12), [[1, 6], [96, 2]], 0, 0)
+    iota(R("lt", 12, 24), [[16, 2], [32, 6]], 0, 0)
+    ts(R("l1"), R("lt", 0, 12), col(12), A.add)
+    ts(R("l2"), R("lt", 12, 24), col(1), A.add)
 
-    def sums(cur):
-        for c in range(3):
-            mms(R("b5", 64 * c, 64 * c + 64), wrap(SUM, cur, 1024 * c, 1024 * c + 1024))
+    def sums(cur, c):
+        mms(R("b5", 64 * c, 64 * c + 64), wrap(SUM, cur, 1024 * c, 1024 * c + 1024))
 
-    sums("xw0")
+    for c in range(3):
+        sums("xw0", c)
 
     def one_round(r):
-        cur, nxt = xw[r % 2], xw[(r + 1) % 2]
+        cur, nxt = xw[r], xw[r + 1]
         last_round = r == RO - 1
         ab = lambda a, b: R(nxt, W + a, W + b)
         full = R(cur, 0, W)
-        tt(R("ee", 0, 1024), X(full, R("pn", 0, 64)), R("xa", 0, 1024), A.subtract)
-        act(R("ee", 2048, V), X(full, R("pn", 128, 192)))
-        tt(R("ee", 1024, 2048), X(full, R("pn", 64, 128)), R("xa", 1024, 2048), A.subtract)
+        ci, ei = R("ci", 0, NC), R("ci", NC, 2 * NC)
+        ts(R("ci", 2 * NC, 3 * NC), R("hi"), 1, A.arith_shift_right, 4095, A.bitwise_and)
+        cp(R("pn"), R("ci", 2 * NC, 3 * NC))
+        ts(ci, R("hi"), 5, A.arith_shift_right, 255, A.bitwise_and)
+        ts(ei, R("hi"), 31, A.bitwise_and)
+        ts(R("hm"), R("hi"), 8191, A.bitwise_and)
+        tt(R("da"), ci, R("ia", 0, NC), A.subtract)
+        ts(R("de"), ei, col(8), A.subtract)
+        act(R("hv"), R("b5", 0, NC), AF.Sign, R("bf", 1, 2))
+        for row, name in enumerate(("da", "de", "hk")):
+            dma("s", R("at", ROFF, ROFF + V, row=row), R(name))
+        mms(R("b2", 0, NC), [(wb(IDN), R("da")), (wb(I216), R("de")), (wb(IDN), R("oc", 0, NC))])
+        ts(R("pl"), R("b2", 0, NC), col(9), A.add)
+        if r:
+            for i in range(16):
+                wipe("pt", S2 * i + SG, S2 * i + SG + NC, 0, "g")
+        dma("s", R("pt", 0, PTW, row=0), R("pbg"), 2.8)
+        for c in range(2):
+            tt(R("dd", 1024 * c, 1024 * c + 1024), X(full, R("pn", 64 * c, 64 * c + 64)), R("xa", 1024 * c, 1024 * c + 1024), A.subtract)
+        act(R("dd", 2048, V), X(full, R("pn", 128, 192)))
         for h in range(2):
-            mms(R("b%d" % h), [(wb(IDN), R("ee", 2048 + 512 * h, 2560 + 512 * h)), (wb(NID), R(cur, 2048 + 512 * h, 2560 + 512 * h))])
-
-        def gapsum(c):
-            mms(R("b4", 64 * c, 64 * c + 64), wrap(SUM, nxt, W + 1024 * c, W + 1024 * c + 1024))
-
-        act(ab(0, 1024), R("ee", 0, 1024), AF.Abs)
-        gapsum(0)
+            mms(R("b%d" % h), [(wb(IDN), R("dd", 2048 + 512 * h, 2560 + 512 * h)), (wb(NID), R(cur, 2048 + 512 * h, 2560 + 512 * h))])
+        act(ab(0, 1024), R("dd", 0, 1024), AF.Abs)
+        mms(R("b4", 0, 64), wrap(SUM, nxt, W, W + 1024))
+        mms(R("b3", 0, 64), wrap(NEG, "dd", 1024, 2048), stop=False)
         for h in range(2):
             act(ab(2048 + 512 * h, 2560 + 512 * h), R("b%d" % h), AF.Abs)
-        gapsum(2)
-        act(ab(1024, 2048), R("ee", 1024, 2048), AF.Abs)
-        gapsum(1)
-        if r:
-            cp(R("hf"), R("b3", 0, NC), True)
-            cp(R("hi"), R("b3", 0, NC))
-        ts(R("ci", 0, NC), R("hi"), 5, A.arith_shift_right)
-        ts(R("ci", SG, SG + NC), R("hi"), 1, A.arith_shift_right, 15, A.bitwise_and)
-        ts(R("ci", 2 * SG, 2 * SG + NC), R("hi"), 1, A.bitwise_and)
-        cp(R("ats"), R("ci", 0, 2 * SG))
-        ts(R("b7", 0, NC), R("ci", 2 * SG, 2 * SG + NC), 2.0, A.mult)
-        tt(R("fls", 0, NC), R("b7", 0, NC), R("hk"), A.add)
-        dma("s", R("at", row=0), R("ats", 0, SG))
-        dma("s", R("at", row=1), R("ats", SG, 2 * SG))
-        dma("s", R("at", row=2), R("fls"))
-        ts(R("hv"), R("b5", 0, NC), R("bf", 1, 2), A.is_ge)
-        if r:
-            tt(R("b4", NC, 2 * NC), R("b4", 0, NC), R("flw", 0, NC), A.add)
-        ts(R("cand"), R("b4", NC if r else 0, 2 * NC if r else NC), R("bf", 0, 1), A.is_ge)
-        mms(R("b2", 0, NC), [(wb(ONE), R("cand"))])
-        mms(R("b0", 0, NC), [(wb(NON), R("cand")), (wb(KW), R("kc"))])
-        mms(R("b6", 0, NC), [(wb(TRV), R("cand")), (wb(KV), R("kc"))])
-        mms(R("b3", 0, NC), [(wb(TRU), R("cand"))])
-        act(R("val"), R("b6", 0, NC))
-        scan(R("cx", 1, NC + 1), R("b2", 0, NC), R("zero", 0, NC), 0.0, A.add, A.add)
-        tt(R("b7", 0, NC), R("b0", 0, NC), R("cx", 0, NC), A.max)
-        tt(R("t2"), R("b7", 0, NC), R("dm"), A.mult)
-        scan(R("t3"), R("hold"), R("t2"), 0.0, A.mult, A.add)
-        cp(R("tl"), R("t3", 15, NC, 16))
-        tt(R("t1"), R("b3", 0, NC), R("cx", 0, NC), A.add)
-        ts(R("b3", 0, NC), R("t1"), 512.0 - 4096.0, A.is_lt)
-        tt(R("sts", 0, NC), R("b3", 0, NC), R("hv"), A.max)
-        dma("s", R("at", row=3), R("sts"))
-        cp(X(R("zz"), R("tl")), R("val"))
-        scan(R("b7"), R("neg"), R("zz", 0, 512), 0.0, A.add, A.max)
-        ts(R("hh"), R("b7"), MAGIC1K, A.add, MAGIC1K, A.subtract)
-        mms(R("b1", 0, 32), wrap(CH, "hh", 0, 512), stop=False)
-        tt(R("mt"), R("b7"), R("hh"), A.is_equal)
-        mms(R("b1", 0, 32), wrap(CM, "mt", 0, 512), start=False)
-        ts(L("ng", 0), R("v16", 0, 32), R("cx", NC, NC + 1), A.is_ge, BIG, A.mult)
-        ts(L("sl", 0), R("b1", 0, 32), -1.0, A.add, float(TW - 1), A.min)
-        mms(R("b6"), [(ws(ZH, 1), R("hh")), (ws(ZM, 1), R("mt"))])
-        tt(Z(0), R("b6"), R("jc"), A.add)
-        for n in range(1, 6):
-            act(Z(n), Z(0), bias=col(24 + n))
-        lo, hi = R("b7", 0, NC), R("b7", NC, 2 * NC)
-        ts(lo, R("hf"), float(2 * V), A.is_lt)
-        tt(R("t4"), lo, R("ci", 2 * SG, 2 * SG + NC), A.mult)
-        ts(lo, R("ci", SG, SG + NC), 384.0, A.mult)
-        tt(hi, lo, R("ci", 0, NC), A.add)
-        tt(lo, hi, R("slf"), A.subtract)
-        tt(hi, lo, R("t4"), A.mult)
-        tt(lo, hi, R("slf"), A.add)
-        cp(R("hl"), lo)
+        ts(ab(1024, 2048), R("dd", 1024, 2048), 0.0, A.max)
+        mms(R("b3", 0, 64), wrap(TWO, nxt, W + 1024, W + 2048), start=False)
+        mms(R("b4", 128, 192), wrap(SUM, nxt, W + 2048, W + V))
+        for c, src in enumerate((R("b4", 0, 64), R("b3", 0, 64), R("b4", 128, 192))):
+            o = R("cc", 208 + 64 * c, 272 + 64 * c)
+            if r:
+                tt(o, src, R("thr", 64 * c, 64 * c + 64), A.is_ge)
+            else:
+                ts(o, src, R("bf", 0, 1), A.is_ge)
+        cand = R("cc", 208, 400)
+        scan(R("cc", 1, NC + 1), R("pos", 0, NC), cand, 0.0, A.mult, A.add)
+        mms(R("b6", 0, NC), [(wb(TRV), cand)])
+        act(R("val"), R("b6", 0, NC), bias=col(5))
+        mms(R("b2", 0, 25), wrap(SUM, "cc", 0, 400) + [(wb(IDN), R("kb", 0, 25))])
+        for bank in ("b3", "b6"):
+            mms(R(bank, 0, NC), [(wb(HVY), R("hv")), (wb(TRU), cand), (wb(ONE), R("cc", 0, NC))])
+        ts(R("tu", 0, 12), R("b2", 13, 25), -4096.0, A.mult, col(10), A.add)
+        tt(R("tu", 16, 28), R("b2", 0, 12), R("tu", 0, 12), A.max)
+        cp(R("tl"), R("tu", 16, 28))
+        z0 = 512 * (RO - 1 - r)
+        cp(X(R("z1", z0, z0 + ZW), R("tl")), R("val"))
+        node({"a": (0.05 + NC * SCAT * CYC, lambda: g.scalar.activation(T.z2[:, z0:z0 + ZW].indirect(T.tl[:, 0:12]), T.cz[:, 0:NC], AF.Silu))},
+             [X(R("z2", z0, z0 + ZW), R("tl"))], [R("cz")])
+        scan(R("s1"), R("neg"), R("z1", z0, z0 + 512), -1.0, A.add, A.max)
+        ts(R("mt"), R("s1"), 0.0, A.is_equal)
+        scan(R("s2"), R("pos"), R("z2", z0, z0 + 512), 0.0, A.mult, A.max)
+        mms(R("b2", 32, 64), wrap(CM, "mt", 0, 512), stop=False)
+        mms(R("b2", 32, 64), wrap(CH, "s2", 0, 512), start=False)
+        ts(L("sl", 0), R("b2", 32, 64), SG - 1.0, A.add)
+        act(R("sns", 0, NC), R("b6", 0, NC), AF.Sign, col(13))
+        ts(R("b7", 0, NC), R("b3", 0, NC), 511.5, A.is_ge)
+        dma("s", R("at", 0, PTW, row=3), R("sns"))
+        for row, name in enumerate(("da", "de", "hk")):
+            tt(R("s" + name, 0, NC), R("b7", 0, NC), R(name), A.mult)
+            dma("s", R("at", 0, PTW, row=row), R("s" + name))
 
         def xgather(k):
             o = R("ee", 6 - k, 3584, 7, cls=k)
@@ -504,145 +558,109 @@ def rank_program(g, core, T, topo):
             if k == 6:
                 cp(o, w, True)
             else:
-                lin(o, w, 0.5, col(30))
+                lin(o, w, 0.5, col(4))
 
-        def addresses(k, n, hk):
-            t = L("ta", k, n)
-            ts(t, L("sl", k, n), 2.0, A.mult, U0 / 2 + 1.0, A.add)
-            if hk is not None:
-                tt(t, t, hk, A.add)
-            tt(t, t, L("mm", k, n), A.max)
-            tt(t, t, L("lv", k + 1, n), A.subtract)
-            tt(t, t, L("dum", 0, n), A.min)
-            ts(L("al", k, n), t, 2.0, A.mult)
-            for m in range(k, k + n):
-                sput(X(R("ut"), L("al", m)), Z(m), True)
-
-        def hold_on(k, src):
-            t = L("tb", k - 1)
-            tt(t, src, L("nf", k - 1), A.subtract)
-            tt(t, t, L("lv", k - 1), A.mult)
-            tt(L("nf", k), t, L("nf", k - 1), A.add)
-            cp(L("nl", k), L("nf", k))
-
-        def logic(k):
-            bank = "b%d" % (2 + k % 2)
-            tt(L("mm", k), R(bank, 0, 32), L("ng", k), A.max)
-            ts(L("lv", k), L("mm", k), BIG, A.is_lt)
-            if k < 5:
-                ts(L("ng", k + 1), L("mm", k), 1.0, A.is_ge, BIG, A.mult)
-            if 1 <= k <= 4:
-                addresses(k - 1, 1, None if last_round or k == 1 else L("mm", k - 2))
-            if k == 5:
-                addresses(4, 2, None if last_round else L("mm", 3, 2))
-            if k:
-                hold_on(k, R(bank, 32, 64))
+        def rung(k, n):
+            if k == 0 and not last_round:
+                pairs = [(st(m), G(j)) for j, m in enumerate((MF0, MN1, Y2, Y2 + 1, Y2 + 2, Y2 + 3))]
             else:
-                cp(L("nf", 0), R(bank, 32, 64))
-                cp(L("nl", 0), R(bank, 32, 64))
-            xgather(k)
+                pairs = [(st(MFP if k == 1 else MF), G(0))]
+                if k >= 2 and not last_round:
+                    pairs.append((st(MP), G(k - 1)))
+                if k < 5:
+                    pairs.append((st(MN), G(k + 1)))
+            bank, s = R("b%d" % (4 + n % 4)), R("src", 512 * (n % 4), 512 * (n % 4) + 512)
+            if len(pairs) > 1:
+                mms(bank, pairs[:-1], stop=False)
+            mms(bank, pairs[-1:], start=len(pairs) == 1)
+            if k == 0 and not last_round:
+                ts(s, bank, R("bt", 6, 7), A.add, col(36), A.max)
+            else:
+                relu(s, bank, R("bt", k, k + 1))
+            sput(X(R("pt"), L("al", k)), s)
 
+        done = 0
         for k in range(6):
-            gk = "g%d" % (k % 2)
-            p1, bank = R("b%d" % (k % 2), 0, 32), "b%d" % (2 + k % 2)
-            cp(R(gk), X(R("at"), L("sl", k)), True)
-            if k < 5:
-                mms(p1, wrap(SIG, gk, 0, 512))
-            mms(R(bank, 0, 32), wrap(FL if k else FL0, gk, 0, 512))
-            mms(R(bank, 32, 64), wrap(NAT, gk, 0, 512))
-            if k == 5:
-                mms(p1, wrap(NP, gk, 0, 512))
             if k:
-                logic(k - 1)
+                cp(G(k), X(R("at"), L("sl", k)), True)
+            else:
+                tt(G(0), X(R("at"), L("sl", 0)), R("jc"), A.add)
             if k < 5:
+                p1 = R("b%d" % (k % 2), 0, 32)
+                mms(p1, wrap(NXT, "gk", 512 * k, 512 * k + 512))
                 cp(L("sl", k + 1), p1)
-        logic(5)
-        hold_on(6, R("b1", 0, 32))
-        xgather(6)
-        dma("s", R("wrp"), urow(0), 3.8)
-        dma("s", R("wrd"), urow(1), 3.8)
+            if k == 0:
+                mms(R("b3", 0, 32), wrap(NTO, "gk", 0, 512))
+                ts(L("nl", 0), R("b3", 0, 32), -0.25, A.add)
+                xgather(0)
+            if k % 2:
+                bank = "b%d" % (2 + k // 2 % 2)
+                mms(R(bank, 0, 64), wrap(UW, "gk", 512 * (k - 1), 512 * (k + 1)))
+                tt(L("ta", k - 1, 2), R(bank, 0, 64), R("dum"), A.min)
+                ts(L("al", k - 1, 2), L("ta", k - 1, 2), BIG, A.add)
+                mms(R(bank, 64, 128), wrap(NTN, "gk", 512 * (k - 1), 512 * (k + 1)))
+                ts(L("nl", k, 2), R(bank, 64, 128), -0.25, A.add)
+                xgather(k)
+                xgather(k + 1)
+            for m in [k - 1] * (k >= (1 if last_round else 2)) + ([5] + [0] * (not last_round)) * (k == 5):
+                rung(m, done)
+                done += 1
+        dma("s", R("po0"), R("pt", 0, PTW, row=0), 2.8)
+        dma("s", R("po2"), R("pt", 0, PTW, row=2), 2.8)
+        for c in range(4):
+            a, b = 896 * c, 896 * c + 896
+            scan(R("uh", a, b), R("half"), R("ee", a, b), 0.0, A.mult, A.add)
+            ts(R(cur, W + a, W + b), R("uh", a, b), MAGIC, A.add, MAGIC, A.subtract)
+        tab = R("pt", 0, PTW)
         if not last_round:
-            t = R("td")
-            ts(t, L("nf", 6), float(V), A.is_lt, BIG, A.mult)
-            tt(t, t, L("nf", 6), A.add)
-            tt(t, t, L("ng", 0), A.add)
+            dma("s", R("po1"), R("pt", 0, PTW, row=1), 2.8)
+            cp(R("sg"), X(tab, R("shp")), True)
+            mms(R("b1", 0, 24), wrap(SW, "sg", 0, 384))
+            tt(R("sf", 0, 24), R("b1", 0, 24), R("sf", 48, 72), A.max)
+            cp(R("shl"), R("sf", 0, 24))
+            cp(R("sh%d" % (r + 1)), X(R(cur), R("shl")), True)
+            send("sh%d" % (r + 1), 0, nxt, V, 1, "sa%d" % (r + 1))
+            t, z = R("td"), R("b2", 96, 128)
+            ts(t, z, float(V), A.is_lt, BIG, A.mult)
+            tt(t, z, t, A.add)
             tt(t, t, R("duf"), A.min)
-            ts(R("fa"), t, -float(V), A.add)
+            ts(R("fa"), t, -V - 0.25, A.add)
             sput(X(R("fw", 896 * r, 896 * r + 896), R("fa")), R("one"))
             send("fw", 896 * r, "fl%d" % r, 0, -1, "fa%d" % r)
-            gfill("zz", 0, 512, 0)
-            tt(R("tc"), L("lv", 0, 6), L("lv", 1, 6), A.subtract)
-            tt(R("tc"), R("tc"), R("mm"), A.mult)
-            tt(L("tc", 0, 3), L("tc", 0, 3), L("tc", 3, 3), A.add)
-            tt(L("tc", 0), L("tc", 0), L("tc", 1), A.add)
-            tt(L("tc", 0), L("tc", 0), L("tc", 2), A.add)
-            ts(L("tc", 1), L("tc", 0), 1.0, A.is_ge)
-            tt(L("tc", 0), L("tc", 1), L("tc", 0), A.subtract)
-            ts(L("tc", 0), L("tc", 0), 0.5, A.add, 2 * BIG, A.mult)
-            ts(L("tc", 3), L("sl", 0), 0.5, A.mult, U0 / 2, A.add)
-            tt(L("tc", 0), L("tc", 0), L("tc", 3), A.add)
-            tt(L("tc", 0), L("tc", 0), L("dum", 0), A.min)
-            ts(R("a0"), L("tc", 0), 2.0, A.mult)
-            if r:
-                dma("s", R("ut", U0, U0 + TW, row=2), R("zero", 0, SG))
-            sput(X(R("ut"), R("a0")), R("one"))
-            dma("s", R("h0"), R("ut", U0, U0 + TW, row=2))
-            dma("s", urow(0), R("zero"), 3.8)
-            dma("s", urow(1), R("zero"), 3.8)
-        scan(R("uh"), R("half"), R("ee"), 0.0, A.mult, A.add)
-        ts(R(cur, W, XWID), R("uh"), MAGIC, A.add, MAGIC, A.subtract)
-        tt(R("b7", 0, 384), R("wrp", 0, 768, 2), R("wrp", 1, 768, 2), A.max)
-        cp(R("t3"), R("b7", 1, 384, 2), True)
-        tt(R("b6", 0, NC), R("b7", 0, 384, 2), R("t3"), A.max)
-        tt(R("b6", NC, 2 * NC), R("b6", 0, NC), R("v16", 0, NC), A.max)
-        cp(R("xl"), R("b6", NC, 2 * NC))
-        for h in range(6):
-            cp(R(nxt, 512 * h, 512 * h + 512), X(R(cur), R("xl", 32 * h, 32 * h + 32)), True)
-        if last_round:
-            for h in range(2):
-                dma("s", hbm(T.y[:, 1536 * h:1536 * h + 1536]), R(nxt, 1536 * h, 1536 * h + 1536), 3.5)
-        else:
-            cp(R("sh%d" % (r + 1)), X(R(nxt, 0, V), R("shn")), True)
-            send("sh%d" % (r + 1), 0, nxt, V, 1, "sa%d" % (r + 1))
-            sums(nxt)
-        lo, hi = R("b4", 0, NC), R("b4", NC, 2 * NC)
-        ts(hi, R("b7", 0, 384, 2), 0.0, A.is_gt)
-        tt(R("t1"), R("wrd", 2, 768, 4), R("wrd", 3, 768, 4), A.max)
-        tt(lo, hi, R("hk"), A.mult)
-        tt(R("hs", NC, 2 * NC), lo, R("hf"), A.add)
-        tt(R("t2"), hi, R("hf"), A.mult)
-        ts(lo, R("t1"), MAGIC, A.add, MAGIC + 64.0, A.subtract)
-        tt(R("t2"), lo, R("t2"), A.max)
-        ts(lo, R("b6", 0, NC), 0.0, A.is_equal)
-        tt(hi, lo, R("k2"), A.mult)
-        tt(R("hs", 0, NC), hi, R("t2"), A.max)
-        if last_round:
-            tab = R("ut", 0, 6144)
-            dma("s", R("ut", 0, 6144, row=0), R("hs"))
-            for h in range(6):
-                cp(R("ut", 6144 + 512 * h, 6656 + 512 * h), X(tab, R("hl", 32 * h, 32 * h + 32)), True)
-            dma("s", hbm(T.yh[:]), R("ut", 6144, 6144 + V, row=0))
-            return
-        cp(R("hsh"), R("hs"), True)
-        dma("s", R("htb", row=0), R("hsh"))
-        tt(R("hsl"), R("hs"), R("hsh"), A.subtract)
-        dma("s", R("htb", row=1), R("hsl"))
-        dma("s", R("xa"), R(nxt, 0, 2048), 4.0)
         for c in range(3):
             for h in (2 * c, 2 * c + 1):
-                cp(ab(512 * h, 512 * h + 512), X(R("htb"), R("hl", 32 * h, 32 * h + 32)), True)
-            mms(R("b3", 64 * c, 64 * c + 64), wrap(SUM, nxt, W + 1024 * c, W + 1024 * c + 1024))
+                cp(R("dd", 512 * h, 512 * h + 512), X(tab, L("pl", h)), True)
+            mms(R("b0", 64 * c, 64 * c + 64), wrap(WW, "dd", 1024 * c, 1024 * c + 1024))
+        cp(R("xl"), odd("po0"))
+        for h in range(6):
+            cp(R(nxt, 512 * h, 512 * h + 512), X(R(cur), L("xl", h)), True)
+            if h % 2 and last_round:
+                dma("s", hbm(T.y[:, 512 * h - 512:512 * h + 512]), R(nxt, 512 * h - 512, 512 * h + 512), 3.0)
+            elif h % 2:
+                sums(nxt, h // 2)
+                if h < 4:
+                    dma("s", R("xa", 512 * h - 512, 512 * h + 512), R(nxt, 512 * h - 512, 512 * h + 512), 2.7)
         lo, hi = R("b7", 0, NC), R("b7", NC, 2 * NC)
-        ts(lo, R("b6", 0, NC), 0.0, A.is_equal)
-        tt(R("t5"), lo, R("hk"), A.mult)
-        tt(R("t6"), R("wrp", 1, 768, 4), R("wrp", 3, 768, 4), A.max)
-        tt(lo, R("t6"), R("t5"), A.max)
-        tt(hi, lo, R("h0", 0, NC), A.max)
-        ts(R("hk"), hi, 0.5, A.is_gt)
+        act(lo, odd("po2"), scale=1.0 / 32)
+        tt(hi, lo, R("hk"), A.mult)
+        tt(R("aa"), hi, R("hm"), A.add)
+        tt(R("hi"), R("b0", 0, NC), R("aa"), A.max)
+        if last_round:
+            ts(R("hm"), R("hi"), 8191, A.bitwise_and)
+            cp(R("y1"), X(R("hm"), R("l1")))
+            node({"v": (NC * CYC, lambda: g.vector.transpose(T.y2[:, :], T.y1[:, :]))}, [R("y2")], [R("y1")])
+            cp(R("y3"), X(R("y2"), R("l2")))
+            for h in range(2):
+                dma("sa"[h], hbm(T.yh[h::2, :]), R("y3", 96 * h, 96 * h + 96))
+            return
+        act(R("thk"), R("hk"), bias=col(7), scale=-20.0)
+        act(R("b3", 0, NC), odd("po1"), AF.Abs, col(6))
+        tt(R("hk"), R("b3", 0, NC), R("thk"), A.is_gt)
         sput(X(R("ft"), R("shs")), R("fl%d" % r))
         dma("s", R("flw"), R("ft", row=0))
-        ts(R("pn"), R("b3", 0, NC), 0.5, A.mult, -0.25, A.add)
+        lin(R("thr"), R("flw"), -1.0, R("bf", 0, 1))
 
+    fill(col(13), -511.5)
     for r in range(RO):
         one_round(r)
     emit()

@@ -6,14 +6,17 @@ V, W, NC, SG, RO = 3072, 3456, 192, 216, 3
 S2 = 2 * SG
 XWID = W + 3584
 PTW = 16 * S2
-ROFF = PTW + 24
-ATW = ROFF + V + 8
+ROFF = PTW + NC
+ATW = ROFF + V
+OFF = 136.0
 ZW = 3264
 BIG = 8192.0
-MAGIC = 12582912.0
-CYC, PEC, GATH, SCAT, WAKE = 1.04e-3, 0.6e-3, 1.56, 3.8, 0.06
-MODELS = (((0.7, 0.45, 0.75, 1.0), 0.88), ((1.0, 1.0, 1.0, 1.0), 1.0), ((1.3, 1.55, 1.6, 1.0), 1.25))
-TRIES = 1500
+CYC, PEC, GATH, SCAT = 1.04e-3, 0.6e-3, 1.56, 3.8
+MODELS = (((0.75, 0.6, 0.9, 0.9, 0.1), 0.95), ((0.83, 0.83, 1.0, 0.83, 0.1), 1.0), ((1.0, 1.0, 1.0, 1.0, 0.08), 1.15),
+          ((1.3, 1.55, 1.4, 1.1, 0.08), 1.45))
+PLANF = (0.95, 0.95, 1.0, 0.95, 0.1)
+TRIES = 300
+MOVES, HEAT = 40000, 0.5
 PLAN = {}
 
 F, B, I, U, H = "float32", "bfloat16", "int32", "uint16", "float16"
@@ -25,9 +28,9 @@ def _s(n, d):
 
 SCRATCH = {
     "xw0": _s(XWID, B), "xw1": _s(XWID, B), "xw2": _s(XWID, B), "at": _s(ATW, B), "pt": _s(PTW + 512, F),
-    "ee": _s(3584, B), "uh": _s(3584, H), "half": _s(896, B), "dd": _s(V, B), "gk": _s(V, B), "src": _s(2048, F),
-    "z1": _s(ZW + 1024, B), "z2": _s(ZW + 1024, F), "ft": _s(V, F), "fw": _s(1792, F), "one": _s(512, F),
-    "fl0": _s(384, F), "fl1": _s(384, F), "flw": _s(NC, F), "thr": _s(NC, F),
+    "ee": _s(3584, H), "half": _s(1792, B), "dd": _s(V, B), "gk": _s(V, B), "src": _s(3072, F), "ft": _s(512, B),
+    "z1": _s(ZW + 1024, B), "z2": _s(ZW + 1024, F), "fw": _s(1792, F), "one": _s(512, F),
+    "fl0": _s(384, F), "fl1": _s(384, F), "flw": _s(S2, F), "thr": _s(NC, F),
     "sh0": _s(384, B), "sh1": _s(384, B), "sh2": _s(384, B), "sg": _s(384, B),
     "po0": _s(S2, F), "po1": _s(S2, F), "po2": _s(S2, F), "pbg": _s(S2, F),
     "jc": _s(512, B), "jt": _s(1024, B), "s1": _s(512, B), "s2": _s(512, B), "mt": _s(512, B), "neg": _s(512, B), "pos": _s(512, B),
@@ -209,64 +212,137 @@ def rank_program(g, core, T, topo):
             g.remote_dma_fused(tr, local_sem=T.sem.sent)
         node({"g": (0.5, make)}, [R(dst, off, off + 384)], [R(src, so, so + 384)], lat=3.0, kind="r", arrive=sem)
 
-    def schedule(prio, lean):
-        left = [len(nd["deps"]) for nd in nodes]
-        free = {q: 0.0 for q in Q}
-        at, done, out = {}, {}, []
-        ready = [n for n in range(len(nodes)) if not left[n]]
-        for n in ready:
-            at[n] = 0.0
-        while ready:
-            best = []
-            for n in ready:
-                o = nodes[n]["opts"]
-                fin, q = min((max(at[n], free[q]) + o[q][0] + (lean[n] if q == "v" else 0.0), q) for q in o)
-                best.append((max(at[n], free[q]), -prio[n], n, q))
-            t0, _, n, q = min(best)
-            end = t0 + nodes[n]["opts"][q][0]
-            for (t1, p1, m, q1) in best:
-                if q1 == q and t1 < end and -p1 > prio[n] and end - p1 > t1 + nodes[m]["opts"][q][0] + prio[n]:
-                    t0, n = t1, m
-                    end = t0 + nodes[n]["opts"][q][0]
-            free[q] = end
-            done[n] = end + nodes[n]["lat"]
-            out.append((n, q))
-            ready.remove(n)
-            for s in succ[n]:
-                left[s] -= 1
-                if not left[s]:
-                    at[s] = max(done[d] for d in nodes[s]["deps"]) + WAKE
-                    ready.append(s)
-        return out
+    def place(key, lean, f, back):
+        nn = len(nodes)
+        busy = {q: [] for q in Q}
+        start, end, where = [0.0] * nn, [0.0] * nn, [None] * nn
+        for n in toposort(key, back):
+            nd = nodes[n]
+            best = None
+            for q, (c, _) in nd["opts"].items():
+                c *= f[nd["sort"]]
+                t = 0.0
+                for d in (succ[n] if back else nd["deps"]):
+                    e = end[d] + (0.0 if q == "p" and where[d] == "p" else f[4]) + (0.0 if back else nodes[d]["lat"])
+                    if e > t:
+                        t = e
+                if back:
+                    t += nd["lat"]
+                b = busy[q]
+                i = len(b)
+                while i and b[i - 1][1] > t:
+                    i -= 1
+                while i < len(b) and b[i][0] < t + c:
+                    t = max(t, b[i][1])
+                    i += 1
+                fin = t + c + (lean[n] if q == "v" else 0.0)
+                if best is None or fin < best[0]:
+                    best = (fin, q, t, t + c, i)
+            _, q, start[n], end[n], i = best
+            busy[q].insert(i, (start[n], end[n]))
+            where[n] = q
+        return start, end, where
 
-    def replay(out, f):
+    def toposort(key, back):
+        key = list(key)
+        for n in (range(len(nodes) - 1, -1, -1) if back else range(len(nodes))):
+            for d in (succ[n] if back else nodes[n]["deps"]):
+                if key[d] >= key[n]:
+                    key[n] = key[d] + 1e-6
+        return sorted(range(len(nodes)), key=lambda n: key[n])
+
+    def replay(out, f, why=None):
         free = {q: 0.0 for q in Q}
-        done = {}
+        done, where, last = [0.0] * len(nodes), [None] * len(nodes), {}
+        wake = f[4]
         for n, q in out:
             nd = nodes[n]
-            t0 = max([free[q]] + [done[d] + WAKE for d in nd["deps"]])
-            free[q] = t0 + nd["opts"][q][0] * f[nd["sort"]]
-            done[n] = free[q] + nd["lat"]
-        return max(done.values())
+            t = free[q]
+            cause = None
+            for d in nd["deps"]:
+                e = done[d] if q == "p" and where[d] == "p" else done[d] + wake
+                if e > t:
+                    t, cause = e, d
+            free[q] = t = t + nd["opts"][q][0] * f[nd["sort"]]
+            done[n] = t + nd["lat"]
+            where[n] = q
+            if why is not None:
+                if cause is not None or q in last:
+                    why[n] = (last[q], True) if cause is None else (cause, False)
+                last[q] = n
+        if why is not None:
+            why["end"] = int(np.argmax(done))
+        return max(done)
 
     def plan():
-        base = [0.0] * len(nodes)
-        for n in range(len(nodes) - 1, -1, -1):
-            base[n] = min(c for c, _ in nodes[n]["opts"].values()) + nodes[n]["lat"] + max([base[s] + WAKE for s in succ[n]] + [0.0])
+        nn = len(nodes)
         rng = np.random.RandomState(7)
-        shift, lean = np.zeros(len(nodes)), np.full(len(nodes), 0.8)
+        f = PLANF
+        key, lean = [float(n) for n in range(nn)], np.full(nn, 0.3)
         best = None
         for it in range(TRIES):
-            s2, l2 = shift.copy(), lean.copy()
-            if it:
-                pick = rng.rand(len(nodes)) < 0.015
-                s2[pick] += rng.randn(int(pick.sum())) * 1.5
-                pick = rng.rand(len(nodes)) < 0.03
-                l2[pick] = rng.randn(int(pick.sum())) * 1.5
-            out = schedule([float(b + s) for b, s in zip(base, s2)], [float(x) for x in l2])
-            score = sum(replay(out, f) / w for f, w in MODELS)
+            l2 = lean.copy()
+            k2 = np.array(key)
+            if it > 3:
+                near = np.abs(k2 - rng.rand() * k2.max()) < 4.0
+                pick = near & (rng.rand(nn) < 0.15)
+                l2[pick] = rng.randn(int(pick.sum()))
+                pick = near & (rng.rand(nn) < 0.15)
+                k2[pick] += rng.randn(int(pick.sum())) * 1.2
+            l2 = [float(x) for x in l2]
+            k2 = [float(x) for x in k2]
+            if it < 4 or it % 8 == 0:
+                _, end, _ = place([-x for x in k2], l2, f, True)
+                k2 = [-x for x in end]
+            start, _, where = place(k2, l2, f, False)
+            out = [(n, where[n]) for n in toposort(start, False)]
+            score = sum(replay(out, m) / w for m, w in MODELS)
             if best is None or score <= best[0]:
-                best, shift, lean = (score, out), s2, l2
+                best, key, lean = (score, out), start, np.array(l2)
+        return polish(best[1], rng)
+
+    def polish(out, rng):
+        score = lambda o: sum(replay(o, m) / w for m, w in MODELS)
+        now = score(out)
+        best = (now, out)
+        pairs = []
+        for it in range(MOVES):
+            if not pairs:
+                why = {}
+                replay(out, MODELS[rng.randint(len(MODELS))][0], why)
+                n = why["end"]
+                while n in why:
+                    if why[n][1]:
+                        pairs.append((why[n][0], n))
+                    n = why[n][0]
+                pos = {n: i for i, (n, q) in enumerate(out)}
+            m, n = pairs[rng.randint(len(pairs))]
+            kind = rng.randint(4)
+            i, j = pos[m], pos[n]
+            if kind < 2:
+                x = (m, n)[kind]
+                other = [q for q in nodes[x]["opts"] if q != out[pos[x]][1]]
+                if not other:
+                    continue
+                new = list(out)
+                new[pos[x]] = (x, other[rng.randint(len(other))])
+            else:
+                if rng.rand() < 0.3:
+                    far = rng.randint(1, 12)
+                    i, j = (max(0, i - far), j) if kind == 2 else (i, min(len(out) - 1, j + far))
+                span = out[i:j + 1]
+                moved = {n if kind == 2 else m}
+                for (x, q) in (reversed(span) if kind == 2 else span):
+                    if any(y in moved for y in (succ[x] if kind == 2 else nodes[x]["deps"])):
+                        moved.add(x)
+                a = [e for e in span if e[0] in moved]
+                b = [e for e in span if e[0] not in moved]
+                new = out[:i] + (a + b if kind == 2 else b + a) + out[j + 1:]
+            s = score(new)
+            if s <= now + HEAT * (1.0 - it / MOVES) * rng.rand():
+                now, out, pairs = s, new, []
+                if s < best[0]:
+                    best = (s, new)
         return best[1]
 
     def emit():
@@ -322,7 +398,7 @@ def rank_program(g, core, T, topo):
 
     SUM, NEG, TWO, NXT, NTN, NTO, UW, CH, CM, WW, SW = range(11)
     IDN, NID, I216, TRV, TRU, ONE, HVY = range(7)
-    MF, MFP, MF0, MN, MN1, MP, Y2 = range(7)
+    MN, MN1, MP, MP5, Y0, Y2 = range(6)
     xw = ["xw0", "xw1", "xw2", "xw0"]
     col = lambda k: R("pc", k, k + 1)
     oh = lambda k: R("oh", k, k + 1)
@@ -331,11 +407,10 @@ def rank_program(g, core, T, topo):
     odd = lambda name: R(name, SG, SG + NC)
 
     dma("s", R("si"), hbm(T.shw[:]))
-    dma("s", R("xw0", 0, V), hbm(T.x[:]), 5.0)
+    dma("s", R("xw1", 0, V), hbm(T.x[:]), 5.0)
     dma("a", R("hi"), hbm(T.hang[:]))
     dma("a", R("ki"), hbm(T.kid[:]))
     dma("a", R("bi", 0, 2), hbm(T.bar[:]))
-    dma("s", R("xa"), hbm(T.x[:, 0:2048]), 7.0)
     iota(R("pi", 0, 1), [[0, 1]], 0, 1)
     iota(R("ia"), [[1, SG]], 0, 0)
     iota(R("ic"), [[16, 8], [0, 16]], 0, 0)
@@ -345,7 +420,9 @@ def rank_program(g, core, T, topo):
     tt(col(2), col(0), col(1), A.subtract)
     ts(col(3), col(2), 15.0, A.add)
     cp(R("shn"), R("si"))
-    cp(R("sh0"), X(R("xw0", 0, V), R("shn")), True)
+    fill(col(14), OFF)
+    fill(col(15), -OFF)
+    lin(R("sh0"), X(R("xw1", 0, V), R("shn")), 1.0, col(14))
     send("sh0", 0, "xw0", V, 1, "sa0")
     ts(R("ew"), R("ia", 0, 144), col(3), A.is_equal)
     ts(R("idn"), R("ia", 0, 128), col(0), A.is_equal)
@@ -369,7 +446,7 @@ def rank_program(g, core, T, topo):
     ts(col(8), col(1), 2.0, A.mult, 1.0, A.add)
     ts(col(9), col(1), float(S2), A.mult, float(SG), A.add)
     ts(col(10), col(1), 12.0, A.mult, float(V), A.add)
-    ts(col(11), col(1), float(NC), A.mult, float(ROFF - SG), A.add)
+    ts(col(11), col(1), float(NC), A.mult, float(NC), A.add)
     ts(col(12), col(1), 6.0, A.mult)
     wset(SUM, 1.0)
     wset(NEG, -1.0)
@@ -402,16 +479,19 @@ def rank_program(g, core, T, topo):
     wcol(31, [(4, 32.0), (3, BIG)])
     wcol(32, [(5, 32.0), (3, BIG)])
     wcol(33, [(2, 128.0), (3, -32.0)])
-    for r, c, w in ((0, col(30), 1.0), (5, oh(4), 32.0), (6, oh(5), 32.0), (7, oh(6), 32.0), (8, oh(7), 32.0)):
-        scol(MF, r, c, w)
-    for r, c, w in ((2, oh(3), 16.0), (11, oh(3), -16.0), (5, oh(3), -BIG), (6, oh(3), -BIG), (3, col(31), 1.0), (4, col(32), 1.0)):
+    wcol(37, [(8, 32.0), (3, -BIG)])
+    wcol(38, [(9, 32.0), (3, -BIG)])
+    wcol(39, [(6, 1.0), (7, 1.0), (8, 1.0), (9, 1.0)])
+    for r, c, w in ((0, col(30), 1.0), (7, oh(6), 32.0), (8, oh(7), 32.0)):
         scol(MN, r, c, w)
-    cp(st(MFP), st(MF), True)
-    cp(st(MF0), st(MF), True)
+        scol(MP5, r, c, w)
+    for r, c, w in ((2, oh(3), 16.0), (11, oh(3), -16.0), (5, col(37), 1.0), (6, col(38), 1.0), (3, col(31), 1.0), (4, col(32), 1.0)):
+        scol(MN, r, c, w)
+    for r, c, w in ((1, oh(2), 64.0), (5, oh(8), 32.0), (6, oh(9), 32.0)):
+        scol(MP5, r, c, w)
     cp(st(MN1), st(MN), True)
-    scol(MFP, 1, oh(2), 64.0)
     scol(MP, 1, oh(2), 64.0)
-    for k, n in enumerate((MF0, MN1, Y2, Y2 + 1, Y2 + 2, Y2 + 3)):
+    for k, n in enumerate((Y0, MN1, Y2, Y2 + 1, Y2 + 2, Y2 + 3)):
         scol(n, 1, col(33), float(2 ** k))
     wcol(34, [(0, W + 6.0), (1, 32.0), (2, 16.0), (3, -BIG), (4, -BIG - 32), (5, -BIG), (6, -BIG - 32), (7, 480.0), (8, 416.0),
               (9, 352.0), (10, 32.0), (11, 16.0)])
@@ -427,12 +507,12 @@ def rank_program(g, core, T, topo):
     for r in range(RO):
         wipe("z1", 512 * r, 512 * r + 512, -1, "v")
         wipe("z2", 512 * r, 512 * r + 512, 32)
-    wipe("ft", 0, V, 0, "gva")
-    wipe("one", 0, 512, 256)
+    lin(col(40), oh(12), 256.0, 0.0)
+    lin(R("one"), R("zero", 0, 512), 0.0, col(40))
     wipe("fw", 0, 384, 0, "gva")
     wipe("fw", 896, 1280, 0, "gva")
     fill(R("half"), 0.5)
-    fill(R("half", 0, 896, 7), 0.0)
+    fill(R("half", 0, 1792, 7), 0.0)
     fill(R("neg"), -1.0)
     fill(R("pos"), 1.0)
     fill(R("jc"), 0.0)
@@ -450,8 +530,11 @@ def rank_program(g, core, T, topo):
         lin(R("oe", SG * h, SG * h + SG), R("ia"), 0.0, col(8))
     dma("s", R("at", 0, PTW, row=4), R("oc"))
     dma("s", R("at", 0, PTW, row=5), R("oe"))
-    dma("s", R("at", ROFF, ROFF + V, row=4), R("oc", 0, NC))
-    dma("s", R("at", ROFF, ROFF + V, row=5), R("oe", 0, NC))
+    for row in (4, 8):
+        dma("s", R("at", ROFF, ROFF + V, row=row), R("oc", 0, NC))
+        dma("s", R("at", ROFF, ROFF + V, row=row + 1), R("oe", 0, NC))
+    for row, name in ((3, "neg"), (4, "oc"), (5, "pos")):
+        dma("s", R("at", PTW, ROFF, row=row), R(name, 0, NC, row=row))
     dma("s", R("at", ROFF, ROFF + V, row=3), R("pos", 0, NC))
     fill(R("cc", 0, 16), 0.0)
     fill(R("cc", NC, NC + 16), 0.0)
@@ -462,12 +545,12 @@ def rank_program(g, core, T, topo):
         ts(L("dum", h), R("v16", 0, 32), PTW - BIG, A.add)
     ts(R("duf"), R("v16", 0, 32), float(W), A.add)
     ts(R("bf", 0, 1), R("bi", 0, 1), -0.5, A.add)
-    ts(R("bf", 1, 2), R("bi", 1, 2), -1.0, A.mult, 0.5, A.add)
+    ts(R("bf", 1, 2), R("bi", 1, 2), -1.0, A.mult, 0.5 - 16 * OFF, A.add)
     ts(R("hk"), R("ki"), float(W), A.is_lt)
     ts(R("sj", 0, 24), R("si"), 15, A.bitwise_and)
     ts(R("sj", 24, 48), R("si"), 4, A.arith_shift_right)
     cp(R("sf", 48, 72), R("si"))
-    ts(R("sf", 0, 24), R("sj", 0, 24), float(NC), A.mult)
+    ts(R("sf", 0, 24), R("sj", 0, 24), float(S2), A.mult)
     ts(R("sf", 24, 48), R("sj", 0, 24), float(S2), A.mult, float(SG), A.add)
     tt(R("sf", 0, 24), R("sf", 0, 24), R("sj", 24, 48), A.add)
     tt(R("sf", 24, 48), R("sf", 24, 48), R("sj", 24, 48), A.add)
@@ -482,7 +565,10 @@ def rank_program(g, core, T, topo):
         mms(R("b5", 64 * c, 64 * c + 64), wrap(SUM, cur, 1024 * c, 1024 * c + 1024))
 
     for c in range(3):
+        lin(R("xw0", 1024 * c, 1024 * c + 1024), R("xw1", 1024 * c, 1024 * c + 1024), 1.0, col(14))
         sums("xw0", c)
+        if c < 2:
+            dma("s", R("xa", 1024 * c, 1024 * c + 1024), R("xw0", 1024 * c, 1024 * c + 1024), 2.7)
 
     def one_round(r):
         cur, nxt = xw[r], xw[r + 1]
@@ -544,7 +630,7 @@ def rank_program(g, core, T, topo):
         scan(R("s2"), R("pos"), R("z2", z0, z0 + 512), 0.0, A.mult, A.max)
         mms(R("b2", 32, 64), wrap(CM, "mt", 0, 512), stop=False)
         mms(R("b2", 32, 64), wrap(CH, "s2", 0, 512), start=False)
-        ts(L("sl", 0), R("b2", 32, 64), SG - 1.0, A.add)
+        ts(L("sl", 0), R("b2", 32, 64), -1.0, A.add)
         act(R("sns", 0, NC), R("b6", 0, NC), AF.Sign, col(13))
         ts(R("b7", 0, NC), R("b3", 0, NC), 511.5, A.is_ge)
         dma("s", R("at", 0, PTW, row=3), R("sns"))
@@ -562,14 +648,12 @@ def rank_program(g, core, T, topo):
 
         def rung(k, n):
             if k == 0 and not last_round:
-                pairs = [(st(m), G(j)) for j, m in enumerate((MF0, MN1, Y2, Y2 + 1, Y2 + 2, Y2 + 3))]
+                pairs = [(st(m), G(j)) for j, m in enumerate((Y0, MN1, Y2, Y2 + 1, Y2 + 2, Y2 + 3))]
+            elif k == 5:
+                pairs = [(st(MP5), G(4))]
             else:
-                pairs = [(st(MFP if k == 1 else MF), G(0))]
-                if k >= 2 and not last_round:
-                    pairs.append((st(MP), G(k - 1)))
-                if k < 5:
-                    pairs.append((st(MN), G(k + 1)))
-            bank, s = R("b%d" % (4 + n % 4)), R("src", 512 * (n % 4), 512 * (n % 4) + 512)
+                pairs = [(st(MP), G(k - 1))] * (not last_round) + [(st(MN), G(k + 1))]
+            bank, s = R("b%d" % (4 + n % 4)), R("src", 512 * n, 512 * n + 512)
             if len(pairs) > 1:
                 mms(bank, pairs[:-1], stop=False)
             mms(bank, pairs[-1:], start=len(pairs) == 1)
@@ -582,9 +666,10 @@ def rank_program(g, core, T, topo):
         done = 0
         for k in range(6):
             if k:
-                cp(G(k), X(R("at"), L("sl", k)), True)
+                tt(G(k), X(R("at", 0, PTW), L("sl", k)), R("ft"), A.add)
             else:
-                tt(G(0), X(R("at"), L("sl", 0)), R("jc"), A.add)
+                tt(G(0), X(R("at", PTW, ATW), L("sl", 0)), R("jc"), A.add)
+                lin(R("ft"), G(0), col(39), 0.0)
             if k < 5:
                 p1 = R("b%d" % (k % 2), 0, 32)
                 mms(p1, wrap(NXT, "gk", 512 * k, 512 * k + 512))
@@ -607,10 +692,8 @@ def rank_program(g, core, T, topo):
                 done += 1
         dma("s", R("po0"), R("pt", 0, PTW, row=0), 2.8)
         dma("s", R("po2"), R("pt", 0, PTW, row=2), 2.8)
-        for c in range(4):
-            a, b = 896 * c, 896 * c + 896
-            scan(R("uh", a, b), R("half"), R("ee", a, b), 0.0, A.mult, A.add)
-            ts(R(cur, W + a, W + b), R("uh", a, b), MAGIC, A.add, MAGIC, A.subtract)
+        for a in (0, 1792):
+            scan(R(cur, W + a, W + a + 1792), R("half"), R("ee", a, a + 1792), 0.0, A.mult, A.add)
         tab = R("pt", 0, PTW)
         if not last_round:
             dma("s", R("po1"), R("pt", 0, PTW, row=1), 2.8)
@@ -633,7 +716,7 @@ def rank_program(g, core, T, topo):
             mms(R("b0", 64 * c, 64 * c + 64), wrap(WW, "dd", 1024 * c, 1024 * c + 1024))
         cp(R("xl"), odd("po0"))
         for h in range(6):
-            cp(R(nxt, 512 * h, 512 * h + 512), X(R(cur), L("xl", h)), True)
+            lin(R(nxt, 512 * h, 512 * h + 512), X(R(cur), L("xl", h)), 1.0, col(15) if last_round else 0.0)
             if h % 2 and last_round:
                 dma("s", hbm(T.y[:, 512 * h - 512:512 * h + 512]), R(nxt, 512 * h - 512, 512 * h + 512), 3.0)
             elif h % 2:
@@ -656,9 +739,9 @@ def rank_program(g, core, T, topo):
         act(R("thk"), R("hk"), bias=col(7), scale=-20.0)
         act(R("b3", 0, NC), odd("po1"), AF.Abs, col(6))
         tt(R("hk"), R("b3", 0, NC), R("thk"), A.is_gt)
-        sput(X(R("ft"), R("shs")), R("fl%d" % r))
-        dma("s", R("flw"), R("ft", row=0))
-        lin(R("thr"), R("flw"), -1.0, R("bf", 0, 1))
+        sput(X(tab, R("shs")), R("fl%d" % r))
+        dma("s", R("flw"), R("pt", 0, PTW, row=12), 2.8)
+        lin(R("thr"), R("flw", 0, NC), -1.0, R("bf", 0, 1))
 
     fill(col(13), -511.5)
     for r in range(RO):

import numpy as np
from concourse.bass import DstId, RemoteDMATransfer
from concourse.mybir import AluOpType, ActivationFunctionType

V, W, NC, SG, RO = 3072, 3456, 192, 216, 3
S2 = 2 * SG
XWID = W + 3584
PTW = 16 * S2
ROFF = PTW + NC
ATW = ROFF + V
OFF = 136.0
ZW = 3264
BIG = 8192.0
CYC, PEC, GATH, SCAT = 1.04e-3, 0.6e-3, 1.56, 3.8
MODELS = (((0.75, 0.6, 0.9, 0.9, 0.1), 0.95), ((0.83, 0.83, 1.0, 0.83, 0.1), 1.0), ((1.0, 1.0, 1.0, 1.0, 0.08), 1.15),
          ((1.3, 1.55, 1.4, 1.1, 0.08), 1.45))
PLANF = (0.95, 0.95, 1.0, 0.95, 0.1)
TRIES = 300
MOVES, HEAT = 40000, 0.5
PLAN = {}

F, B, I, U, H = "float32", "bfloat16", "int32", "uint16", "float16"


def _s(n, d):
    return ("sbuf", [128, n], d)


SCRATCH = {
    "xw0": _s(XWID, B), "xw1": _s(XWID, B), "xw2": _s(XWID, B), "at": _s(ATW, B), "pt": _s(PTW + 512, F),
    "ee": _s(3584, H), "half": _s(1792, B), "dd": _s(V, B), "gk": _s(V, B), "src": _s(3072, F), "ft": _s(512, B),
    "z1": _s(ZW + 1024, B), "z2": _s(ZW + 1024, F), "fw": _s(1792, F), "one": _s(512, F),
    "fl0": _s(384, F), "fl1": _s(384, F), "flw": _s(S2, F), "thr": _s(NC, F),
    "sh0": _s(384, B), "sh1": _s(384, B), "sh2": _s(384, B), "sg": _s(384, B),
    "po0": _s(S2, F), "po1": _s(S2, F), "po2": _s(S2, F), "pbg": _s(S2, F),
    "jc": _s(512, B), "jt": _s(1024, B), "s1": _s(512, B), "s2": _s(512, B), "mt": _s(512, B), "neg": _s(512, B), "pos": _s(512, B),
    "zero": _s(1024, B), "xa": _s(2048, B),
    "hi": _s(NC, I), "ki": _s(NC, I), "ci": _s(3 * NC, I), "hm": _s(NC, I), "si": _s(24, I), "sj": _s(48, I), "sf": _s(72, F),
    "bi": _s(8, I), "bf": _s(8, F), "shn": _s(24, U), "shs": _s(24, U), "shp": _s(24, U), "shl": _s(24, U),
    "pn": _s(NC, U), "pl": _s(NC, U), "xl": _s(NC, U), "tl": _s(12, U), "l1": _s(12, U), "l2": _s(12, U),
    "da": _s(NC, B), "de": _s(NC, B), "hk": _s(NC, B), "hv": _s(NC, B), "val": _s(NC, B), "cz": _s(NC, F),
    "sda": _s(S2, B), "sde": _s(S2, B), "shk": _s(S2, B), "sns": _s(S2, B), "oc": _s(S2, B), "oe": _s(S2, B),
    "aa": _s(NC, F), "thk": _s(NC, F), "cc": _s(400, B), "kb": _s(32, B), "tu": _s(32, F),
    "y1": _s(NC, F), "y2": _s(NC, F), "y3": _s(NC, F),
    "pi": _s(8, I), "pc": _s(48, F), "bt": _s(8, F), "oh": _s(16, F), "ia": _s(SG, F), "ic": _s(128, F), "v16": _s(SG, F),
    "ew": _s(144, F), "wset": _s(144 * 11, B), "bo": _s(128, F), "tri": _s(128, F), "idn": _s(128, F), "tmp": _s(256, F),
    "wblk": _s(128 * 8, B), "st": _s(128 * 10, B),
    "sl": _s(192, U), "nl": _s(224, U), "al": _s(192, U), "fa": _s(32, U),
    "ta": _s(192, F), "td": _s(32, F), "dum": _s(64, F), "duf": _s(32, F), "lt": _s(24, F),
}
for _k in range(8):
    SCRATCH["b%d" % _k] = ("psum", [128, 512], F)
NDMA = 70
SEMAPHORES = ["cv", "ca", "cp", "cg", "sent", "sa0", "sa1", "sa2", "fa0", "fa1"] + ["d%d" % _k for _k in range(NDMA)]


def rank_program(g, core, T, topo):
    rank = T.rank_of(core)
    if rank is None:
        return
    N = len(T.cores)
    A = AluOpType
    AF = ActivationFunctionType
    Q = {"v": g.vector, "a": g.scalar, "p": g.tensor, "g": g, "s": g.sync}
    hist = {}
    nodes = []
    succ = []

    def R(name, a=None, b=None, s=None, row=None, cls=None):
        t = T[name]
        a = 0 if a is None else a
        b = t.shape[1] if b is None else b
        cs = slice(a, b) if s is None else slice(a, b, s)
        pat = t[:, cs] if row is None else t[row::16, cs]
        n = len(range(a, b, s or 1))
        if SCRATCH[name][0] == "psum":
            return (pat, [(name, 0, 512, "psum")], None, n, 4, True)
        return (pat, [(name, a, b, row if cls is None else cls)], None, n, 4 if SCRATCH[name][2] in (F, I) else 2, False)

    def X(win, off):
        return (win[0].indirect(off[0]), win[1], off[1], 16 * off[3], win[4], False)

    def hbm(t):
        return (t, [], None, 0, 0, False)

    def ap(o):
        return o[0] if isinstance(o, tuple) else o

    def node(opts, outs, ins, lat=0.0, kind="c", arrive=None):
        reads, writes = [], []
        for o in ins:
            if isinstance(o, tuple):
                reads += o[1] + (o[2] or [])
        for o in outs:
            writes += o[1]
            reads += o[2] or []
        me = len(nodes)
        qs = "".join(opts)
        deps = set()
        for regs, wr in ((reads, False), ([] if arrive else writes, True)):
            for (n, a, b, cls) in regs:
                for (a2, b2, cls2, wr2, qs2, who) in hist.get(n, []):
                    if a2 >= b or a >= b2:
                        continue
                    if cls == "psum":
                        if not (wr or wr2 or qs2 != qs or len(qs) > 1):
                            continue
                    elif not (wr or wr2) or (cls is not None and cls2 is not None and cls != cls2):
                        continue
                    deps.add(who)
        sort = 2 if qs == "p" else 1 if outs[0][2] else 0 if ins and isinstance(ins[0], tuple) and ins[0][2] else 3
        nodes.append({"sort": sort, "opts": opts, "lat": lat, "kind": kind, "deps": sorted(deps), "arrive": arrive})
        for (n, a, b, cls) in writes:
            h = [e for e in hist.get(n, []) if not (a <= e[0] and e[1] <= b and (cls is None or cls == e[2]))]
            hist[n] = h + [(a, b, cls, True, qs, me)]
        for (n, a, b, cls) in reads:
            hist[n] = hist.get(n, []) + [(a, b, cls, False, qs, me)]

    def vcost(out, ins, per):
        if out[2]:
            return 0.05 + out[3] * SCAT * CYC
        if ins and ins[0][2]:
            return 0.05 + out[3] * GATH * CYC
        return max(64, out[3] * per) * CYC

    def half(*o):
        return 0.5 if all(x[4] == 2 for x in o) else 1.0

    def aopt(out, in_, f, bias, scale):
        return (vcost(out, [in_], 1.0) + 0.02, lambda: g.scalar.activation(out[0], in_[0], f, ap(bias), ap(scale)))

    def cp(out, in_, either=False):
        opts = {"v": (vcost(out, [in_], half(out, in_)), lambda: g.vector.tensor_copy(out[0], in_[0]))}
        if either:
            opts["a"] = aopt(out, in_, AF.Identity, 0.0, 1.0)
        node(opts, [out], [in_])

    def lin(out, in_, scale, bias):
        node({"v": (vcost(out, [in_], half(out, in_)), lambda: g.vector.tensor_scalar(out[0], in_[0], ap(scale), ap(bias), A.mult, A.add)),
              "a": aopt(out, in_, AF.Identity, bias, scale)}, [out], [in_, scale, bias])

    def relu(out, in_, bias):
        node({"v": (vcost(out, [in_], 1.0), lambda: g.vector.tensor_scalar(out[0], in_[0], bias[0], 0.0, A.add, A.max)),
              "a": aopt(out, in_, AF.Relu, bias, 1.0)}, [out], [in_, bias])

    def tt(out, a, b, op):
        node({"v": (vcost(out, [a], 1.0 if a[5] or b[5] else 2.0), lambda: g.vector.tensor_tensor(out[0], a[0], b[0], op))}, [out], [a, b])

    def ts(out, a, s1, op0, s2=None, op1=None):
        c = vcost(out, [a], half(out, a))
        if op1 is None:
            node({"v": (c, lambda: g.vector.tensor_scalar(out[0], a[0], ap(s1), None, op0))}, [out], [a, s1])
        else:
            node({"v": (c, lambda: g.vector.tensor_scalar(out[0], a[0], ap(s1), ap(s2), op0, op1))}, [out], [a, s1, s2])

    def scan(out, d0, d1, init, op0, op1):
        node({"v": (vcost(out, [], half(out, d0, d1)), lambda: g.vector.tensor_tensor_scan(out[0], d0[0], d1[0], ap(init), op0, op1))},
             [out], [d0, d1, init])

    def fill(out, c):
        node({"v": (vcost(out, [], half(out)), lambda: g.vector.memset(out[0], c))}, [out], [])

    def act(out, in_, func=None, bias=0.0, scale=1.0):
        node({"a": aopt(out, in_, AF.Identity if func is None else func, bias, scale)}, [out], [in_, bias, scale])

    def sput(o, z):
        node({"a": (vcost(o, [z], 1.0), lambda: g.scalar.activation(o[0], z[0], AF.Silu)),
              "v": (vcost(o, [z], 1.0), lambda: g.vector.tensor_copy(o[0], z[0]))}, [o], [z])

    def iopt(out, pattern, base, mult):
        c = 0.13 + 2 * out[3] * CYC
        if SCRATCH[out[1][0][0]][2] == I:
            return (c, lambda: g.iota(out[0], pattern, base, mult))
        return (c, lambda: g.iota(out[0], pattern, base, mult, allow_small_or_imprecise_dtypes=True))

    def iota(out, pattern, base, mult):
        node({"g": iopt(out, pattern, base, mult)}, [out], [])

    def wipe(name, a, b, c, qs="gv", step=512):
        for lo in range(a, b, step):
            o = R(name, lo, min(b, lo + step))
            opts = {}
            if "g" in qs:
                opts["g"] = iopt(o, [[0, o[3]]], c, 0)
            if "v" in qs:
                opts["v"] = (vcost(o, [], half(o)), lambda o=o: g.vector.memset(o[0], float(c)))
            if "a" in qs:
                opts["a"] = aopt(o, R("zero", 0, o[3]), AF.Identity, 0.0, 1.0)
            node(opts, [o], [R("zero", 0, o[3])] if "a" in qs else [])

    def mms(out, pairs, start=True, stop=True):
        def make():
            for n, (l, r) in enumerate(pairs):
                ins = g.tensor.matmul(out[0], l[0], r[0], start and n == 0, stop and n == len(pairs) - 1)
            return ins
        node({"p": (sum(max(64, r[3]) for (l, r) in pairs) * PEC, make)}, [out], [x for pr in pairs for x in pr])

    def dma(q, out, in_, lat=2.4):
        node({q: (0.1, lambda: Q[q].dma_start(out[0], in_[0]))}, [out], [in_], lat=lat, kind="d")

    def send(src, so, dst, off, sign, sem):
        def make():
            tr = []
            for d in range(1, N):
                peer = T.cores[(rank + sign * d) % N]
                rid, pid = topo.addr(peer, core)
                e = topo.engines(core, peer)
                pick = ((0, 2), (4, 6), (1, 5))[d - 1]
                tr.append(RemoteDMATransfer(dst_ids=[DstId(rid=rid, pnc=pid)], dma_engine_mask=(1 << e[pick[0]]) | (1 << e[pick[1]]),
                                            remote_sem=T.sem[sem], src=T[src][:, so + (d - 1) * 128:so + d * 128],
                                            dst=T[dst][:, off + (d - 1) * 128:off + d * 128]))
            g.remote_dma_fused(tr, local_sem=T.sem.sent)
        node({"g": (0.5, make)}, [R(dst, off, off + 384)], [R(src, so, so + 384)], lat=3.0, kind="r", arrive=sem)

    def place(key, lean, f, back):
        nn = len(nodes)
        busy = {q: [] for q in Q}
        start, end, where = [0.0] * nn, [0.0] * nn, [None] * nn
        for n in toposort(key, back):
            nd = nodes[n]
            best = None
            for q, (c, _) in nd["opts"].items():
                c *= f[nd["sort"]]
                t = 0.0
                for d in (succ[n] if back else nd["deps"]):
                    e = end[d] + (0.0 if q == "p" and where[d] == "p" else f[4]) + (0.0 if back else nodes[d]["lat"])
                    if e > t:
                        t = e
                if back:
                    t += nd["lat"]
                b = busy[q]
                i = len(b)
                while i and b[i - 1][1] > t:
                    i -= 1
                while i < len(b) and b[i][0] < t + c:
                    t = max(t, b[i][1])
                    i += 1
                fin = t + c + (lean[n] if q == "v" else 0.0)
                if best is None or fin < best[0]:
                    best = (fin, q, t, t + c, i)
            _, q, start[n], end[n], i = best
            busy[q].insert(i, (start[n], end[n]))
            where[n] = q
        return start, end, where

    def toposort(key, back):
        key = list(key)
        for n in (range(len(nodes) - 1, -1, -1) if back else range(len(nodes))):
            for d in (succ[n] if back else nodes[n]["deps"]):
                if key[d] >= key[n]:
                    key[n] = key[d] + 1e-6
        return sorted(range(len(nodes)), key=lambda n: key[n])

    def replay(out, f, why=None):
        free = {q: 0.0 for q in Q}
        done, where, last = [0.0] * len(nodes), [None] * len(nodes), {}
        wake = f[4]
        for n, q in out:
            nd = nodes[n]
            t = free[q]
            cause = None
            for d in nd["deps"]:
                e = done[d] if q == "p" and where[d] == "p" else done[d] + wake
                if e > t:
                    t, cause = e, d
            free[q] = t = t + nd["opts"][q][0] * f[nd["sort"]]
            done[n] = t + nd["lat"]
            where[n] = q
            if why is not None:
                if cause is not None or q in last:
                    why[n] = (last[q], True) if cause is None else (cause, False)
                last[q] = n
        if why is not None:
            why["end"] = int(np.argmax(done))
        return max(done)

    def plan():
        nn = len(nodes)
        rng = np.random.RandomState(7)
        f = PLANF
        key, lean = [float(n) for n in range(nn)], np.full(nn, 0.3)
        best = None
        for it in range(TRIES):
            l2 = lean.copy()
            k2 = np.array(key)
            if it > 3:
                near = np.abs(k2 - rng.rand() * k2.max()) < 4.0
                pick = near & (rng.rand(nn) < 0.15)
                l2[pick] = rng.randn(int(pick.sum()))
                pick = near & (rng.rand(nn) < 0.15)
                k2[pick] += rng.randn(int(pick.sum())) * 1.2
            l2 = [float(x) for x in l2]
            k2 = [float(x) for x in k2]
            if it < 4 or it % 8 == 0:
                _, end, _ = place([-x for x in k2], l2, f, True)
                k2 = [-x for x in end]
            start, _, where = place(k2, l2, f, False)
            out = [(n, where[n]) for n in toposort(start, False)]
            score = sum(replay(out, m) / w for m, w in MODELS)
            if best is None or score <= best[0]:
                best, key, lean = (score, out), start, np.array(l2)
        return polish(best[1], rng)

    def polish(out, rng):
        score = lambda o: sum(replay(o, m) / w for m, w in MODELS)
        now = score(out)
        best = (now, out)
        pairs = []
        for it in range(MOVES):
            if not pairs:
                why = {}
                replay(out, MODELS[rng.randint(len(MODELS))][0], why)
                n = why["end"]
                while n in why:
                    if why[n][1]:
                        pairs.append((why[n][0], n))
                    n = why[n][0]
                pos = {n: i for i, (n, q) in enumerate(out)}
            m, n = pairs[rng.randint(len(pairs))]
            kind = rng.randint(4)
            i, j = pos[m], pos[n]
            if kind < 2:
                x = (m, n)[kind]
                other = [q for q in nodes[x]["opts"] if q != out[pos[x]][1]]
                if not other:
                    continue
                new = list(out)
                new[pos[x]] = (x, other[rng.randint(len(other))])
            else:
                if rng.rand() < 0.3:
                    far = rng.randint(1, 12)
                    i, j = (max(0, i - far), j) if kind == 2 else (i, min(len(out) - 1, j + far))
                span = out[i:j + 1]
                moved = {n if kind == 2 else m}
                for (x, q) in (reversed(span) if kind == 2 else span):
                    if any(y in moved for y in (succ[x] if kind == 2 else nodes[x]["deps"])):
                        moved.add(x)
                a = [e for e in span if e[0] in moved]
                b = [e for e in span if e[0] not in moved]
                new = out[:i] + (a + b if kind == 2 else b + a) + out[j + 1:]
            s = score(new)
            if s <= now + HEAT * (1.0 - it / MOVES) * rng.rand():
                now, out, pairs = s, new, []
                if s < best[0]:
                    best = (s, new)
        return best[1]

    def emit():
        for n, nd in enumerate(nodes):
            succ.append([])
            for d in nd["deps"]:
                succ[d].append(n)
        if "order" not in PLAN:
            PLAN["order"] = plan()
        where, mark, final = {}, {}, {}
        cnt = {q: 0 for q in Q}
        seen = {q: {} for q in Q}
        ndma = nsent = 0
        for n, q in PLAN["order"]:
            nd = nodes[n]
            need = {}
            for d in nd["deps"]:
                if not (q == "p" and where[d] == "p"):
                    need[mark[d][0]] = max(need.get(mark[d][0], 0), mark[d][1])
            for sem in need:
                if seen[q].get(sem, 0) < need[sem]:
                    Q[q].wait_ge(T.sem[sem], need[sem])
                    seen[q][sem] = need[sem]
            ins = nd["opts"][q][1]()
            if nd["kind"] == "c":
                cnt[q] += 1
                mark[n] = ("c" + q, cnt[q])
                ins.then_inc(T.sem["c" + q], 1)
            elif nd["kind"] == "d":
                mark[n] = ("d%d" % ndma, 16)
                ins.then_inc(T.sem["d%d" % ndma], 16)
                ndma += 1
            else:
                mark[n] = (nd["arrive"], 2 * (N - 1))
                nsent += 2 * (N - 1)
                final["sent"] = nsent
            final[mark[n][0]] = mark[n][1]
            where[n] = q
        for sem in final:
            g.wait_ge(T.sem[sem], final[sem])

    def ws(n, i):
        return R("wset", 144 * n + 15 - i, 144 * n + 143 - i)

    def wb(n):
        return R("wblk", 128 * n, 128 * n + 128)

    def st(n):
        return R("st", 128 * n, 128 * n + 128)

    def wrap(n, name, a, b):
        return [(ws(n, i), R(name, a + i, b, 16)) for i in range(16)]

    SUM, NEG, TWO, NXT, NTN, NTO, UW, CH, CM, WW, SW = range(11)
    IDN, NID, I216, TRV, TRU, ONE, HVY = range(7)
    MN, MN1, MP, MP5, Y0, Y2 = range(6)
    xw = ["xw0", "xw1", "xw2", "xw0"]
    col = lambda k: R("pc", k, k + 1)
    oh = lambda k: R("oh", k, k + 1)
    L = lambda name, k, n=1: R(name, 32 * k, 32 * (k + n))
    G = lambda k, n=1: R("gk", 512 * k, 512 * (k + n))
    odd = lambda name: R(name, SG, SG + NC)

    dma("s", R("si"), hbm(T.shw[:]))
    dma("s", R("xw1", 0, V), hbm(T.x[:]), 5.0)
    dma("a", R("hi"), hbm(T.hang[:]))
    dma("a", R("ki"), hbm(T.kid[:]))
    dma("a", R("bi", 0, 2), hbm(T.bar[:]))
    iota(R("pi", 0, 1), [[0, 1]], 0, 1)
    iota(R("ia"), [[1, SG]], 0, 0)
    iota(R("ic"), [[16, 8], [0, 16]], 0, 0)
    fill(R("zero"), 0.0)
    ts(R("pi", 1, 2), R("pi", 0, 1), 15, A.bitwise_and)
    cp(R("pc", 0, 2), R("pi", 0, 2))
    tt(col(2), col(0), col(1), A.subtract)
    ts(col(3), col(2), 15.0, A.add)
    cp(R("shn"), R("si"))
    fill(col(14), OFF)
    fill(col(15), -OFF)
    lin(R("sh0"), X(R("xw1", 0, V), R("shn")), 1.0, col(14))
    send("sh0", 0, "xw0", V, 1, "sa0")
    ts(R("ew"), R("ia", 0, 144), col(3), A.is_equal)
    ts(R("idn"), R("ia", 0, 128), col(0), A.is_equal)
    ts(R("oh"), R("ia", 0, 16), col(1), A.is_equal)
    ts(R("bo"), R("ic"), col(2), A.is_equal)
    ts(R("tri"), R("ia", 0, 128), col(0), A.is_gt)
    tt(R("tri"), R("tri"), R("bo"), A.mult)

    def wcol(k, terms):
        lin(col(k), oh(terms[0][0]), terms[0][1], 0.0)
        for (r, w) in terms[1:]:
            lin(col(k), oh(r), w, col(k))

    def wset(n, scale):
        lin(R("wset", 144 * n, 144 * n + 144), R("ew"), scale, 0.0)

    fill(col(4), -0.25)
    fill(col(5), -17.0)
    fill(col(6), -32.0)
    fill(col(7), 40.0)
    ts(col(8), col(1), 2.0, A.mult, 1.0, A.add)
    ts(col(9), col(1), float(S2), A.mult, float(SG), A.add)
    ts(col(10), col(1), 12.0, A.mult, float(V), A.add)
    ts(col(11), col(1), float(NC), A.mult, float(NC), A.add)
    ts(col(12), col(1), 6.0, A.mult)
    wset(SUM, 1.0)
    wset(NEG, -1.0)
    wset(TWO, 2.0)
    wset(CM, col(11))
    lin(wb(IDN), R("idn"), 1.0, 0.0)
    lin(wb(NID), R("idn"), -1.0, 0.0)
    lin(wb(I216), R("idn"), float(SG), 0.0)
    lin(wb(HVY), R("idn"), -4096.0, 0.0)
    lin(wb(ONE), R("bo"), 1.0, 0.0)
    lin(R("tmp", 0, 128), R("idn"), 17.0, 0.0)
    tt(wb(TRV), R("tmp", 0, 128), R("tri"), A.add)
    lin(R("tmp", 128, 256), R("idn"), -4096.0, 0.0)
    tt(wb(TRU), R("tmp", 128, 256), R("tri"), A.add)
    for n, terms in ((NXT, [(0, 1.0), (4, 1.0), (1, float(SG)), (5, float(SG))]), (NTO, [(4, 16.0), (5, 0.5)]),
                     (UW, [(4, 1.0), (5, float(SG)), (3, -BIG)]), (CH, [(0, 1.0 / 32)]),
                     (WW, [(3, 1.0), (5, 1.0), (4, 1.0 / 32), (6, 1.0 / 32), (11, 1.0 / 32), (10, BIG / 32)]),
                     (SW, [(7, 7.0), (8, 7.0 / 32), (9, 1.0 / 32)])):
        wcol(16 + n, terms)
        wset(n, col(16 + n))
    lin(col(16 + NTN), oh(0), 16.0, col(16 + NTO))
    lin(col(16 + NTN), oh(1), 0.5, col(16 + NTN))
    wset(NTN, col(16 + NTN))
    wipe("st", 0, 1280, 0, "va")

    def scol(n, r, c, w=1.0):
        ts(R("st", 128 * n + r, 128 * n + 128, 16, cls=r), R("bo", 0, 128, 16), c, A.mult, w, A.mult)

    wcol(30, [(6, 224.0), (7, 7.0)])
    wcol(31, [(4, 32.0), (3, BIG)])
    wcol(32, [(5, 32.0), (3, BIG)])
    wcol(33, [(2, 128.0), (3, -32.0)])
    wcol(37, [(8, 32.0), (3, -BIG)])
    wcol(38, [(9, 32.0), (3, -BIG)])
    wcol(39, [(6, 1.0), (7, 1.0), (8, 1.0), (9, 1.0)])
    for r, c, w in ((0, col(30), 1.0), (7, oh(6), 32.0), (8, oh(7), 32.0)):
        scol(MN, r, c, w)
        scol(MP5, r, c, w)
    for r, c, w in ((2, oh(3), 16.0), (11, oh(3), -16.0), (5, col(37), 1.0), (6, col(38), 1.0), (3, col(31), 1.0), (4, col(32), 1.0)):
        scol(MN, r, c, w)
    for r, c, w in ((1, oh(2), 64.0), (5, oh(8), 32.0), (6, oh(9), 32.0)):
        scol(MP5, r, c, w)
    cp(st(MN1), st(MN), True)
    scol(MP, 1, oh(2), 64.0)
    for k, n in enumerate((Y0, MN1, Y2, Y2 + 1, Y2 + 2, Y2 + 3)):
        scol(n, 1, col(33), float(2 ** k))
    wcol(34, [(0, W + 6.0), (1, 32.0), (2, 16.0), (3, -BIG), (4, -BIG - 32), (5, -BIG), (6, -BIG - 32), (7, 480.0), (8, 416.0),
              (9, 352.0), (10, 32.0), (11, 16.0)])
    wcol(35, [(0, -1.0), (9, -32.0)])
    lin(R("bt", 0, 6), R("ia", 0, 6), col(35), col(34))
    lin(R("bt", 6, 7), oh(1), -2016.0, R("bt", 0, 1))
    for r, w in ((2, -16.0), (5, BIG), (6, BIG), (11, 16.0)):
        lin(R("bt", 5, 6), oh(r), w, R("bt", 5, 6))
    lin(col(36), oh(1), 32.0, 0.0)

    wipe("at", 0, ATW, 0, "gva", 1024)
    wipe("pt", 0, PTW, 0, "gva")
    for r in range(RO):
        wipe("z1", 512 * r, 512 * r + 512, -1, "v")
        wipe("z2", 512 * r, 512 * r + 512, 32)
    lin(col(40), oh(12), 256.0, 0.0)
    lin(R("one"), R("zero", 0, 512), 0.0, col(40))
    wipe("fw", 0, 384, 0, "gva")
    wipe("fw", 896, 1280, 0, "gva")
    fill(R("half"), 0.5)
    fill(R("half", 0, 1792, 7), 0.0)
    fill(R("neg"), -1.0)
    fill(R("pos"), 1.0)
    fill(R("jc"), 0.0)
    iota(R("jt", 0, 512), [[1, 16], [0, 32]], 0, 0)
    iota(R("jt", 512, 1024), [[0, 16], [1, 32]], 0, 0)
    dma("s", R("jc", row=6), R("jt", 0, 512, row=6))
    dma("s", R("jc", row=7), R("jt", 512, 1024, row=7))
    for name, c in (("sda", 0.0), ("sde", 0.0), ("shk", 0.0), ("sns", -1.0)):
        fill(R(name, NC, S2), c)
    lin(R("v16"), R("ia"), 16.0, col(1))
    fill(R("pbg", 0, SG), 0.0)
    cp(R("pbg", SG, S2), R("v16"), True)
    for h in range(2):
        cp(R("oc", SG * h, SG * h + SG), R("ia"), True)
        lin(R("oe", SG * h, SG * h + SG), R("ia"), 0.0, col(8))
    dma("s", R("at", 0, PTW, row=4), R("oc"))
    dma("s", R("at", 0, PTW, row=5), R("oe"))
    for row in (4, 8):
        dma("s", R("at", ROFF, ROFF + V, row=row), R("oc", 0, NC))
        dma("s", R("at", ROFF, ROFF + V, row=row + 1), R("oe", 0, NC))
    for row, name in ((3, "neg"), (4, "oc"), (5, "pos")):
        dma("s", R("at", PTW, ROFF, row=row), R(name, 0, NC, row=row))
    dma("s", R("at", ROFF, ROFF + V, row=3), R("pos", 0, NC))
    fill(R("cc", 0, 16), 0.0)
    fill(R("cc", NC, NC + 16), 0.0)
    fill(R("kb", 0, 13), 0.0)
    lin(R("kb", 13, 25), R("ia", 0, 12), -1.0 / 4096, 0.0)
    ts(R("cz"), R("ia", 0, NC), 1.0, A.add, 32.0, A.mult)
    for h in range(2):
        ts(L("dum", h), R("v16", 0, 32), PTW - BIG, A.add)
    ts(R("duf"), R("v16", 0, 32), float(W), A.add)
    ts(R("bf", 0, 1), R("bi", 0, 1), -0.5, A.add)
    ts(R("bf", 1, 2), R("bi", 1, 2), -1.0, A.mult, 0.5 - 16 * OFF, A.add)
    ts(R("hk"), R("ki"), float(W), A.is_lt)
    ts(R("sj", 0, 24), R("si"), 15, A.bitwise_and)
    ts(R("sj", 24, 48), R("si"), 4, A.arith_shift_right)
    cp(R("sf", 48, 72), R("si"))
    ts(R("sf", 0, 24), R("sj", 0, 24), float(S2), A.mult)
    ts(R("sf", 24, 48), R("sj", 0, 24), float(S2), A.mult, float(SG), A.add)
    tt(R("sf", 0, 24), R("sf", 0, 24), R("sj", 24, 48), A.add)
    tt(R("sf", 24, 48), R("sf", 24, 48), R("sj", 24, 48), A.add)
    cp(R("shs"), R("sf", 0, 24))
    cp(R("shp"), R("sf", 24, 48))
    iota(R("lt", 0, 12), [[1, 6], [96, 2]], 0, 0)
    iota(R("lt", 12, 24), [[16, 2], [32, 6]], 0, 0)
    ts(R("l1"), R("lt", 0, 12), col(12), A.add)
    ts(R("l2"), R("lt", 12, 24), col(1), A.add)

    def sums(cur, c):
        mms(R("b5", 64 * c, 64 * c + 64), wrap(SUM, cur, 1024 * c, 1024 * c + 1024))

    for c in range(3):
        lin(R("xw0", 1024 * c, 1024 * c + 1024), R("xw1", 1024 * c, 1024 * c + 1024), 1.0, col(14))
        sums("xw0", c)
        if c < 2:
            dma("s", R("xa", 1024 * c, 1024 * c + 1024), R("xw0", 1024 * c, 1024 * c + 1024), 2.7)

    def one_round(r):
        cur, nxt = xw[r], xw[r + 1]
        last_round = r == RO - 1
        ab = lambda a, b: R(nxt, W + a, W + b)
        full = R(cur, 0, W)
        ci, ei = R("ci", 0, NC), R("ci", NC, 2 * NC)
        ts(R("ci", 2 * NC, 3 * NC), R("hi"), 1, A.arith_shift_right, 4095, A.bitwise_and)
        cp(R("pn"), R("ci", 2 * NC, 3 * NC))
        ts(ci, R("hi"), 5, A.arith_shift_right, 255, A.bitwise_and)
        ts(ei, R("hi"), 31, A.bitwise_and)
        ts(R("hm"), R("hi"), 8191, A.bitwise_and)
        tt(R("da"), ci, R("ia", 0, NC), A.subtract)
        ts(R("de"), ei, col(8), A.subtract)
        act(R("hv"), R("b5", 0, NC), AF.Sign, R("bf", 1, 2))
        for row, name in enumerate(("da", "de", "hk")):
            dma("s", R("at", ROFF, ROFF + V, row=row), R(name))
        mms(R("b2", 0, NC), [(wb(IDN), R("da")), (wb(I216), R("de")), (wb(IDN), R("oc", 0, NC))])
        ts(R("pl"), R("b2", 0, NC), col(9), A.add)
        if r:
            for i in range(16):
                wipe("pt", S2 * i + SG, S2 * i + SG + NC, 0, "g")
        dma("s", R("pt", 0, PTW, row=0), R("pbg"), 2.8)
        for c in range(2):
            tt(R("dd", 1024 * c, 1024 * c + 1024), X(full, R("pn", 64 * c, 64 * c + 64)), R("xa", 1024 * c, 1024 * c + 1024), A.subtract)
        act(R("dd", 2048, V), X(full, R("pn", 128, 192)))
        for h in range(2):
            mms(R("b%d" % h), [(wb(IDN), R("dd", 2048 + 512 * h, 2560 + 512 * h)), (wb(NID), R(cur, 2048 + 512 * h, 2560 + 512 * h))])
        act(ab(0, 1024), R("dd", 0, 1024), AF.Abs)
        mms(R("b4", 0, 64), wrap(SUM, nxt, W, W + 1024))
        mms(R("b3", 0, 64), wrap(NEG, "dd", 1024, 2048), stop=False)
        for h in range(2):
            act(ab(2048 + 512 * h, 2560 + 512 * h), R("b%d" % h), AF.Abs)
        ts(ab(1024, 2048), R("dd", 1024, 2048), 0.0, A.max)
        mms(R("b3", 0, 64), wrap(TWO, nxt, W + 1024, W + 2048), start=False)
        mms(R("b4", 128, 192), wrap(SUM, nxt, W + 2048, W + V))
        for c, src in enumerate((R("b4", 0, 64), R("b3", 0, 64), R("b4", 128, 192))):
            o = R("cc", 208 + 64 * c, 272 + 64 * c)
            if r:
                tt(o, src, R("thr", 64 * c, 64 * c + 64), A.is_ge)
            else:
                ts(o, src, R("bf", 0, 1), A.is_ge)
        cand = R("cc", 208, 400)
        scan(R("cc", 1, NC + 1), R("pos", 0, NC), cand, 0.0, A.mult, A.add)
        mms(R("b6", 0, NC), [(wb(TRV), cand)])
        act(R("val"), R("b6", 0, NC), bias=col(5))
        mms(R("b2", 0, 25), wrap(SUM, "cc", 0, 400) + [(wb(IDN), R("kb", 0, 25))])
        for bank in ("b3", "b6"):
            mms(R(bank, 0, NC), [(wb(HVY), R("hv")), (wb(TRU), cand), (wb(ONE), R("cc", 0, NC))])
        ts(R("tu", 0, 12), R("b2", 13, 25), -4096.0, A.mult, col(10), A.add)
        tt(R("tu", 16, 28), R("b2", 0, 12), R("tu", 0, 12), A.max)
        cp(R("tl"), R("tu", 16, 28))
        z0 = 512 * (RO - 1 - r)
        cp(X(R("z1", z0, z0 + ZW), R("tl")), R("val"))
        node({"a": (0.05 + NC * SCAT * CYC, lambda: g.scalar.activation(T.z2[:, z0:z0 + ZW].indirect(T.tl[:, 0:12]), T.cz[:, 0:NC], AF.Silu))},
             [X(R("z2", z0, z0 + ZW), R("tl"))], [R("cz")])
        scan(R("s1"), R("neg"), R("z1", z0, z0 + 512), -1.0, A.add, A.max)
        ts(R("mt"), R("s1"), 0.0, A.is_equal)
        scan(R("s2"), R("pos"), R("z2", z0, z0 + 512), 0.0, A.mult, A.max)
        mms(R("b2", 32, 64), wrap(CM, "mt", 0, 512), stop=False)
        mms(R("b2", 32, 64), wrap(CH, "s2", 0, 512), start=False)
        ts(L("sl", 0), R("b2", 32, 64), -1.0, A.add)
        act(R("sns", 0, NC), R("b6", 0, NC), AF.Sign, col(13))
        ts(R("b7", 0, NC), R("b3", 0, NC), 511.5, A.is_ge)
        dma("s", R("at", 0, PTW, row=3), R("sns"))
        for row, name in enumerate(("da", "de", "hk")):
            tt(R("s" + name, 0, NC), R("b7", 0, NC), R(name), A.mult)
            dma("s", R("at", 0, PTW, row=row), R("s" + name))

        def xgather(k):
            o = R("ee", 6 - k, 3584, 7, cls=k)
            w = X(full, L("nl", k))
            if k == 6:
                cp(o, w, True)
            else:
                lin(o, w, 0.5, col(4))

        def rung(k, n):
            if k == 0 and not last_round:
                pairs = [(st(m), G(j)) for j, m in enumerate((Y0, MN1, Y2, Y2 + 1, Y2 + 2, Y2 + 3))]
            elif k == 5:
                pairs = [(st(MP5), G(4))]
            else:
                pairs = [(st(MP), G(k - 1))] * (not last_round) + [(st(MN), G(k + 1))]
            bank, s = R("b%d" % (4 + n % 4)), R("src", 512 * n, 512 * n + 512)
            if len(pairs) > 1:
                mms(bank, pairs[:-1], stop=False)
            mms(bank, pairs[-1:], start=len(pairs) == 1)
            if k == 0 and not last_round:
                ts(s, bank, R("bt", 6, 7), A.add, col(36), A.max)
            else:
                relu(s, bank, R("bt", k, k + 1))
            sput(X(R("pt"), L("al", k)), s)

        done = 0
        for k in range(6):
            if k:
                tt(G(k), X(R("at", 0, PTW), L("sl", k)), R("ft"), A.add)
            else:
                tt(G(0), X(R("at", PTW, ATW), L("sl", 0)), R("jc"), A.add)
                lin(R("ft"), G(0), col(39), 0.0)
            if k < 5:
                p1 = R("b%d" % (k % 2), 0, 32)
                mms(p1, wrap(NXT, "gk", 512 * k, 512 * k + 512))
                cp(L("sl", k + 1), p1)
            if k == 0:
                mms(R("b3", 0, 32), wrap(NTO, "gk", 0, 512))
                ts(L("nl", 0), R("b3", 0, 32), -0.25, A.add)
                xgather(0)
            if k % 2:
                bank = "b%d" % (2 + k // 2 % 2)
                mms(R(bank, 0, 64), wrap(UW, "gk", 512 * (k - 1), 512 * (k + 1)))
                tt(L("ta", k - 1, 2), R(bank, 0, 64), R("dum"), A.min)
                ts(L("al", k - 1, 2), L("ta", k - 1, 2), BIG, A.add)
                mms(R(bank, 64, 128), wrap(NTN, "gk", 512 * (k - 1), 512 * (k + 1)))
                ts(L("nl", k, 2), R(bank, 64, 128), -0.25, A.add)
                xgather(k)
                xgather(k + 1)
            for m in [k - 1] * (k >= (1 if last_round else 2)) + ([5] + [0] * (not last_round)) * (k == 5):
                rung(m, done)
                done += 1
        dma("s", R("po0"), R("pt", 0, PTW, row=0), 2.8)
        dma("s", R("po2"), R("pt", 0, PTW, row=2), 2.8)
        for a in (0, 1792):
            scan(R(cur, W + a, W + a + 1792), R("half"), R("ee", a, a + 1792), 0.0, A.mult, A.add)
        tab = R("pt", 0, PTW)
        if not last_round:
            dma("s", R("po1"), R("pt", 0, PTW, row=1), 2.8)
            cp(R("sg"), X(tab, R("shp")), True)
            mms(R("b1", 0, 24), wrap(SW, "sg", 0, 384))
            tt(R("sf", 0, 24), R("b1", 0, 24), R("sf", 48, 72), A.max)
            cp(R("shl"), R("sf", 0, 24))
            cp(R("sh%d" % (r + 1)), X(R(cur), R("shl")), True)
            send("sh%d" % (r + 1), 0, nxt, V, 1, "sa%d" % (r + 1))
            t, z = R("td"), R("b2", 96, 128)
            ts(t, z, float(V), A.is_lt, BIG, A.mult)
            tt(t, z, t, A.add)
            tt(t, t, R("duf"), A.min)
            ts(R("fa"), t, -V - 0.25, A.add)
            sput(X(R("fw", 896 * r, 896 * r + 896), R("fa")), R("one"))
            send("fw", 896 * r, "fl%d" % r, 0, -1, "fa%d" % r)
        for c in range(3):
            for h in (2 * c, 2 * c + 1):
                cp(R("dd", 512 * h, 512 * h + 512), X(tab, L("pl", h)), True)
            mms(R("b0", 64 * c, 64 * c + 64), wrap(WW, "dd", 1024 * c, 1024 * c + 1024))
        cp(R("xl"), odd("po0"))
        for h in range(6):
            lin(R(nxt, 512 * h, 512 * h + 512), X(R(cur), L("xl", h)), 1.0, col(15) if last_round else 0.0)
            if h % 2 and last_round:
                dma("s", hbm(T.y[:, 512 * h - 512:512 * h + 512]), R(nxt, 512 * h - 512, 512 * h + 512), 3.0)
            elif h % 2:
                sums(nxt, h // 2)
                if h < 4:
                    dma("s", R("xa", 512 * h - 512, 512 * h + 512), R(nxt, 512 * h - 512, 512 * h + 512), 2.7)
        lo, hi = R("b7", 0, NC), R("b7", NC, 2 * NC)
        act(lo, odd("po2"), scale=1.0 / 32)
        tt(hi, lo, R("hk"), A.mult)
        tt(R("aa"), hi, R("hm"), A.add)
        tt(R("hi"), R("b0", 0, NC), R("aa"), A.max)
        if last_round:
            ts(R("hm"), R("hi"), 8191, A.bitwise_and)
            cp(R("y1"), X(R("hm"), R("l1")))
            node({"v": (NC * CYC, lambda: g.vector.transpose(T.y2[:, :], T.y1[:, :]))}, [R("y2")], [R("y1")])
            cp(R("y3"), X(R("y2"), R("l2")))
            for h in range(2):
                dma("sa"[h], hbm(T.yh[h::2, :]), R("y3", 96 * h, 96 * h + 96))
            return
        act(R("thk"), R("hk"), bias=col(7), scale=-20.0)
        act(R("b3", 0, NC), odd("po1"), AF.Abs, col(6))
        tt(R("hk"), R("b3", 0, NC), R("thk"), A.is_gt)
        sput(X(tab, R("shs")), R("fl%d" % r))
        dma("s", R("flw"), R("pt", 0, PTW, row=12), 2.8)
        lin(R("thr"), R("flw", 0, NC), -1.0, R("bf", 0, 1))

    fill(col(13), -511.5)
    for r in range(RO):
        one_round(r)
    emit()
